import numpy as np, ml_dtypes
CORES = [3,11,19,27,35,43]
N = 6
BF = ml_dtypes.bfloat16
def gentries(a):
    return np.ascontiguousarray(a.reshape(8, 16, -1).transpose(0, 2, 1)).reshape(8, -1)
def gtable(e):
    e = np.asarray(e); return np.ascontiguousarray(e.reshape(8, -1, 16).transpose(0, 2, 1)).reshape(128, -1).astype(np.int32)
H, W, P = 32, 128, 4096
A, B, Q = 16, 32, 512
SW = 1
def pack(F, U, S, J):
    return {"fr": np.ascontiguousarray(F).reshape(N, 128, P).astype(np.float32).astype(BF), "qu": np.ascontiguousarray(U).reshape(N, 128, Q).astype(np.float32).astype(BF),
            "st": np.stack([gtable(v) for v in S]), "ju": np.stack([gtable(v) for v in J])}
def jumps(rng):
    n = (N, 8, SW * Q)
    return np.where(rng.random(n) < 0.5, rng.integers(-2, 3, n) * W + rng.integers(-2, 3, n), rng.integers(1 - P, P, n))
def scene(rng):
    base = rng.integers(0, 16, (8, 16, H, W)); dy = np.add.accumulate(rng.integers(-1, 2, (N, 8)), axis=0); dx = np.add.accumulate(rng.integers(-1, 2, (N, 8)), axis=0)
    F = np.zeros((N, 8, 16, H, W), np.int64); U = np.zeros((N, 8, 16, A, B), np.int64); S = np.zeros((N, 8, Q), np.int64)
    for r in range(N):
        for g in range(8):
            F[r, g] = np.roll(base[g], (int(dy[r, g]), int(dx[r, g])), axis=(1, 2))
            yy = (rng.integers(0, H) + np.arange(A)) % H; xx = (rng.integers(0, W) + np.arange(B)) % W
            U[r, g] = base[g][:, yy][:, :, xx]
            S[r, g] = (((yy + dy[r, g]) % H)[:, None] * W + ((xx + dx[r, g]) % W)[None, :]).reshape(-1)
    F = np.where(rng.random(F.shape) < 0.1, rng.integers(0, 16, F.shape), F); U = np.where(rng.random(U.shape) < 0.2, rng.integers(0, 16, U.shape), U)
    S = np.where(rng.random(S.shape) < 0.1, S, rng.integers(0, P, S.shape))
    return F.reshape(N, 8, 16, P), U.reshape(N, 8, 16, Q), S, jumps(rng)
def setup_inputs(rng):
    return pack(*scene(rng))
def setup_inputs_ties(rng):
    pat = rng.integers(0, 16, (8, 13, 16)); g = np.arange(8)[None, :, None]
    sub = np.argsort(rng.random((N, 8, 12)), axis=-1)[..., :6]
    idx = np.take_along_axis(sub, rng.integers(0, 6, (N, 8, P)), axis=-1)
    F = pat[g, idx].transpose(0, 1, 3, 2); U = pat[g, rng.integers(0, 13, (N, 8, Q))].transpose(0, 1, 3, 2)
    return pack(F, U, rng.integers(0, P, (N, 8, Q)), jumps(rng))
def setup_inputs_edges(rng):
    F, U, S, J = scene(rng)
    S = rng.choice(np.array([0, 1, H - 2, H - 1]), S.shape) * W + rng.choice(np.array([0, 1, W - 2, W - 1]), S.shape)
    J = rng.choice(np.array([0, 1, -1, W, -W, W - 1, P - 1, 1 - P]), J.shape)
    return pack(F, U, S, J)
def setup_inputs_far(rng):
    F = 15 * rng.integers(0, 2, (N, 8, 16, P)); U = 15 * rng.integers(0, 2, (N, 8, 16, Q)); h = rng.integers(0, 8)
    F[:, h] = 15; U[:, h] = 0
    return pack(F, U, rng.integers(0, P, (N, 8, Q)), jumps(rng))
def setup_inputs_one(rng):
    F, U, S, J = scene(rng)
    S = np.zeros_like(S) + rng.integers(0, P, (N, 8, 1)); J = np.zeros_like(J) + rng.integers(1 - P, P, (N, 8, 1))
    J[rng.integers(0, N)] = 0; k = rng.integers(0, N); F[k] = F[k][:, :, :1]
    return pack(F, U, S, J)
def setup_inputs_spread(rng):
    def uneven(n):
        e = np.exp2(rng.integers(-2, 4, (N, 8, 1, n))); v = np.minimum(np.floor(16 * rng.random((N, 8, 16, n)) ** e), 15)
        return v * (rng.random((N, 8, 1, n)) > 0.0625)
    F = uneven(P); U = uneven(Q)
    S = np.minimum(np.floor(P * rng.random((N, 8, Q)) ** 3), P - 1).astype(np.int64); S[:, :, 5] = P - 1
    J = rng.integers(1 - P, P, (N, 8, SW * Q)); J[:, :, 0] = P - 1; J[:, :, 1] = 1 - P
    return pack(F, U, S, J)
def check_inputs(d):
    bad = []
    for nm in ("fr", "qu"):
        v = d[nm].astype(np.float32)
        if not (np.isfinite(v).all() and (v == np.floor(v)).all() and v.min() >= 0 and v.max() <= 15): bad.append(nm)
    if d["st"].min() < 0 or d["st"].max() > P - 1: bad.append("st")
    if d["ju"].min() < 1 - P or d["ju"].max() > P - 1: bad.append("ju")
    return bad
def sides(p, t):
    i = np.arange(Q)
    a = np.roll(p, 1, axis=1); b = np.roll(p, B, axis=1)
    return np.where(i % B > 0, a + (a % W < W - 1), p), np.where(i >= B, np.where(b + W < P, b + W, b), p)
def reference(fr, qu, st, ju):
    F = fr.astype(np.int32).reshape(N, 8, 16, P); U = qu.astype(np.int32).reshape(N, 8, 16, Q)
    yc = np.zeros((N, 128, Q // 16), np.float32); yf = np.zeros_like(yc); yp = np.zeros_like(yc)
    for r in range(N):
        p = gentries(st[r]).astype(np.int64)
        bc = np.full((8, Q), 1 << 20, np.int64); bf = np.zeros((8, Q), np.int64); bp = np.zeros((8, Q), np.int64)
        for s in range(N):
            k = (r + s) % N; J = gentries(ju[k]).astype(np.int64).reshape(8, SW, Q)
            for t in range(SW):
                one, two = sides(p, t)
                c = np.stack([p, one, two, np.minimum(np.maximum(p + J[:, t], 0), P - 1)], axis=1)
                v = np.take_along_axis(F[k], c.reshape(8, 1, 4 * Q), axis=2).reshape(8, 16, 4, Q) - U[r][:, :, None, :]
                e = np.sum(v * v, axis=1); w = np.argmin(e, axis=1)[:, None]
                p = np.take_along_axis(c, w, axis=1)[:, 0]; best = np.take_along_axis(e, w, axis=1)[:, 0]
            m = best < bc
            bc = np.where(m, best, bc); bf = np.where(m, k, bf); bp = np.where(m, p, bp)
        yc[r] = gtable(bc); yf[r] = gtable(bf); yp[r] = gtable(bp)
    return {"yc": yc, "yf": yf, "yp": yp}

@@ -1,0 +1,565 @@
+import math
+from concourse.mybir import AluOpType, AxisListType, ActivationFunctionType
+
+N = 6
+DELTA = [0, 2, 2, 4, 4, 0]
+CH = [(0, 16), (16, 32)]
+WAYS = "fnFn"
+ROUNDS = 40000
+FW = 4224
+TW = 72
+BIG = 8192.0
+EST = {"cy": 1.0e-3, "ga": 1.56, "pe": 0.5e-3, "wake": 0.08, "hop": 2.5, "frame": 12.0, "next": 5.0}
+SPREAD = [{}, {"cy": 0.85e-3, "ga": 1.2, "pe": 0.43e-3}, {"cy": 1.2e-3, "ga": 1.9, "pe": 0.6e-3}, {"pe": 0.9e-3}, {"hop": 3.5, "wake": 0.15}]
+
+NCH = len(CH)
+NPC = len(WAYS)
+FOFF = sorted(set((s - DELTA[s]) % N for s in range(N)))
+UOFF = sorted(set(DELTA))
+JOFF = sorted(set([0] + [(s + 1 - DELTA[s]) % N for s in range(N - 1)]))
+PW = FW // NPC
+
+SCRATCH = {
+    "U": ("sbuf", [128, len(UOFF), 512], "bfloat16"),
+    "ST": ("sbuf", [128, 36], "int32"),
+    "JI": ("sbuf", [128, len(JOFF), 32], "int32"),
+    "C4": ("sbuf", [128, 128], "bfloat16"),
+    "C6": ("sbuf", [128, 2, 192], "bfloat16"),
+    "T0": ("sbuf", [128, N, 32], "float32"),
+    "OFF": ("sbuf", [128, N * NCH * TW], "uint16"),
+    "OFS": ("sbuf", [128, N * NCH * TW], "uint16"),
+    "O1": ("sbuf", [128, N * 32], "uint16"),
+    "PH": ("sbuf", [128, N * NCH * TW], "float16"),
+    "P1H": ("sbuf", [128, N * 32], "float16"),
+    "FL": ("sbuf", [128, N * 96], "bfloat16"),
+    "D": ("sbuf", [128, N * 4 * 512], "bfloat16"),
+    "SQ4": ("sbuf", [128, 32, 64], "bfloat16"),
+    "SQ6": ("sbuf", [128, 32, 96], "bfloat16"),
+    "M": ("sbuf", [128, N, 192], "float32"),
+    "NE": ("sbuf", [128, N, 192], "float32"),
+    "R": ("sbuf", [128, N, 208], "float32"),
+    "RF": ("sbuf", [128, 192], "float32"),
+    "M4": ("sbuf", [128, 4, 128], "float32"),
+    "F4": ("sbuf", [128, 128], "float32"),
+    "RS4": ("sbuf", [128, 128], "float32"),
+    "RS6": ("sbuf", [128, 192], "float32"),
+    "KC4": ("sbuf", [128, 128], "bfloat16"),
+    "KC6": ("sbuf", [128, 192], "bfloat16"),
+    "SC": ("sbuf", [128, 3, 32], "bfloat16"),
+    "HS": ("sbuf", [128, N, 64], "float32"),
+    "HL": ("sbuf", [128, N, 64], "float32"),
+    "Y": ("sbuf", [128, 3, 32], "float32"),
+    "A": ("sbuf", [128, 3, 128], "float32"),
+    "E": ("sbuf", [128, 4, 8], "float32"),
+    "Z": ("sbuf", [128, 144], "bfloat16"),
+    "WH": ("sbuf", [128, 5, 128], "float16"),
+    "WB": ("sbuf", [128, 4, 128], "bfloat16"),
+    "WF": ("sbuf", [128, 2, 128], "float32"),
+}
+for _e in FOFF:
+    SCRATCH["FR%d" % _e] = ("sbuf", [128, FW], "bfloat16")
+for _b in range(8):
+    SCRATCH["B%d" % _b] = ("psum", [128, 512], "float32")
+
+SEMAPHORES = (["cv", "cs", "ct", "cg", "ls"] + ["d%d" % i for i in range(24)]
+              + ["ao%d_%d" % (s, k) for s in range(N) for k in range(NCH)]
+              + ["ah%d_%d" % (s, k) for s in range(N) for k in range(NCH)]
+              + ["au%d" % e for e in UOFF] + ["aj%d" % e for e in JOFF]
+              + ["af%d_%d" % (e, p) for e in FOFF for p in range(NPC)])
+
+ALU = AluOpType
+ACT = ActivationFunctionType
+KEPT = {}
+
+
+def bits(engs):
+    m = 0
+    for e in engs:
+        m |= 1 << e
+    return m
+
+
+def frame_order():
+    out = []
+    for s in range(N):
+        e = (s - DELTA[s]) % N
+        if e and e not in out:
+            out.append(e)
+    return out
+
+
+def forwarders(T, topo, q):
+    c = T.cores[q]
+    dsts = [T.cores[(q - e) % N] for e in frame_order()]
+    ok = [h for h in topo.cores_of(c) if T.rank_of(h) is None and all(topo.may_write(h, d) for d in dsts)]
+    far = [h for h in ok if topo.die(h) != topo.die(c)]
+    near = [h for h in ok if topo.die(h) == topo.die(c)]
+    hs = [{"f": far[0], "F": far[-1], "n": near[0]}[x] for x in WAYS]
+    return hs, [y for y in topo.engines(c, hs[0]) if y not in topo.engines(c, dsts[0])]
+
+
+def helper_program(g, core, T, topo):
+    sent = 0
+    for q in range(N):
+        hs, on = forwarders(T, topo, q)
+        for x, e in enumerate(frame_order()):
+            dst = T.cores[(q - e) % N]
+            rid, pid, _ = topo.addr(dst)
+            for p in range(NPC):
+                if hs[p] != core:
+                    continue
+                if x == 0:
+                    g.wait_ge(T.sem["af0_%d" % p], len(on))
+                g.remote_dma(T["FR%d" % e][:, p * PW:(p + 1) * PW], T.FR0[:, p * PW:(p + 1) * PW], T.sem["af%d_%d" % (e, p)],
+                             T.sem.ls, pid, rid, topo.mask(core, dst))
+                sent += len(topo.engines(core, dst))
+    if sent:
+        g.wait_ge(T.sem.ls, sent)
+
+
+def times(o, est):
+    fix, what, n = o["cost"]
+    dur = fix + n * {"c": est["cy"], "g": est["cy"] * est["ga"], "p": est["pe"]}[what]
+    return dur, (est["hop"] if o["lat"] is None else o["lat"]), (est["frame"] + o["at"] * est["next"] if o["at"] is not None else 0.0)
+
+
+def schedule(ops, est, lead):
+    n = len(ops)
+    wake = est["wake"]
+    tm = [times(o, est) for o in ops]
+    succ = [[] for _ in range(n)]
+    for i, o in enumerate(ops):
+        for d in o["deps"] + o["after"]:
+            succ[d].append(i)
+    pr = [0.0] * n
+    for i in range(n - 1, -1, -1):
+        pr[i] = tm[i][0] + tm[i][1] + max([pr[j] + wake for j in succ[i]] + [0.0])
+    for i in range(n):
+        if ops[i]["tag"] == 0:
+            pr[i] += lead
+    left = [len(o["deps"]) + len(o["after"]) for o in ops]
+    ready = [0.0] * n
+    free = {}
+    seq = []
+    avail = [i for i in range(n) if left[i] == 0]
+    while avail:
+        best = None
+        for i in avail:
+            st = max(ready[i], free.get(ops[i]["eng"], 0.0)) if ops[i]["eng"] else ready[i]
+            if best is None or st < best[0]:
+                best = (st, ops[i]["eng"])
+        t0, eng = best
+        i = max([i for i in avail if ops[i]["eng"] == eng and ready[i] <= t0 + 0.2], key=lambda j: (pr[j], -j))
+        st = max(t0, ready[i])
+        if eng:
+            free[eng] = st + tm[i][0]
+        fin = max(st + tm[i][0] + tm[i][1], tm[i][2])
+        seq.append(i)
+        avail.remove(i)
+        for j in succ[i]:
+            ready[j] = max(ready[j], fin + wake if i in ops[j]["deps"] else st + tm[i][0])
+            left[j] -= 1
+            if left[j] == 0:
+                avail.append(j)
+    return seq
+
+
+def play(seq, ops, tm, wake):
+    fin, st, free = [0.0] * len(ops), [0.0] * len(ops), {}
+    for i in seq:
+        o = ops[i]
+        e = o["eng"]
+        t = free.get(e, 0.0) if e else 0.0
+        for d in o["deps"]:
+            if fin[d] + wake > t:
+                t = fin[d] + wake
+        a, b, c = tm[i]
+        st[i] = t
+        fin[i] = t + a + b if t + a + b > c else c
+        if e:
+            free[e] = t + a
+    return max(fin), st
+
+
+def improve(ops):
+    n = len(ops)
+    cases = []
+    for kw in SPREAD:
+        est = dict(EST)
+        est.update(kw)
+        cases.append(([times(o, est) for o in ops], est["wake"]))
+
+    def cost(s):
+        return sum(play(s, ops, tm, wk)[0] for tm, wk in cases) / len(cases)
+
+    pre = [set(o["deps"] + o["after"]) for o in ops]
+    cur, seq = min((cost(s), s) for s in [schedule(ops, EST, 0.25 * d) for d in range(14)])
+    best, kept = cur, seq
+    x = [12345]
+
+    def rnd(m):
+        x[0] = (x[0] * 1103515245 + 12345) % 2147483648
+        return (x[0] >> 8) % m
+
+    for it in range(ROUNDS):
+        if it % 300 == 0:
+            st = play(seq, ops, cases[0][0], cases[0][1])[1]
+            pos = {j: k for k, j in enumerate(seq)}
+            seq = sorted(seq, key=lambda j: (round(st[j], 6), pos[j]))
+        a = rnd(n)
+        e = ops[seq[a]]["eng"]
+        if e is None:
+            continue
+        k, way, b, seen, grp = [1, 1, 1, 2, 3, 5][rnd(6)], 2 * rnd(2) - 1, a, 0, [seq[a]]
+        while seen < k:
+            b += way
+            if b < 0 or b >= n:
+                break
+            j = seq[b]
+            if any(j in pre[y] for y in grp) if way < 0 else any(y in pre[j] for y in grp):
+                if ops[j]["eng"] == e:
+                    break
+                grp.append(j)
+            elif ops[j]["eng"] == e:
+                seen += 1
+        if seen < k:
+            continue
+        lo, hi = min(a, b), max(a, b)
+        mine, rest = [m for m in seq[lo:hi + 1] if m in grp], [m for m in seq[lo:hi + 1] if m not in grp]
+        c = seq[:lo] + (mine + rest if way < 0 else rest + mine) + seq[hi + 1:]
+        v = cost(c)
+        if v <= cur or rnd(1000000) < 1000000 * math.exp((cur - v) / (0.03 * (1 - it / ROUNDS) + 1e-4)):
+            seq, cur = c, v
+            if v < best:
+                best, kept = v, c
+    return kept
+
+
+def build(g, core, T, topo, rank):
+    ops = []
+    nd = [0]
+    sent = [0]
+    tag = [None]
+    prev = {}
+
+    def flat(x):
+        out = []
+        for d in x:
+            if isinstance(d, (list, tuple)):
+                out += flat(d)
+            elif d is not None:
+                out.append(d)
+        return out
+
+    def add(eng, fn, cost, deps=(), after=(), kind="c", lat=0.0, sem=None, val=0, at=None):
+        ops.append({"eng": eng, "fn": fn, "cost": cost, "deps": sorted(set(flat(deps))), "after": sorted(set(flat(after))),
+                    "kind": kind, "lat": lat, "sem": sem, "val": val, "at": at, "tag": tag[0]})
+        return len(ops) - 1
+
+    def V(fn, n, deps=(), gather=False):
+        return add("v", fn, (0.05, "g", n) if gather else (0.0, "c", max(n, 64)), deps)
+
+    def S(fn, n, deps=(), gather=False):
+        return add("s", fn, (0.065, "g", n) if gather else (0.03, "c", max(n, 64)), deps)
+
+    def MM(lst, deps=(), after=()):
+        def fn(q):
+            for (o, w, x, a, b) in lst:
+                ins = q.matmul(o, w, x, a, b)
+            return ins
+        cyc = 0
+        for (o, w, x, a, b) in lst:
+            cyc += max(64, list(o.shape)[1]) * (4 if "32" in str(w.dtype) else 1)
+        return add("t", fn, (0.0, "p", cyc), deps, after)
+
+    def DMA(eng, out, in_, deps=(), lat=2.0):
+        name = "d%d" % nd[0]
+        nd[0] += 1
+        prev[eng] = add(eng, lambda q: q.dma_start(out, in_), (0.1, "c", 0), deps, [prev.get(eng)], kind="d", lat=lat, sem=name, val=16)
+        return prev[eng]
+
+    def WRITE(dst, out, in_, sem, deps, engs, after=()):
+        rid, pid, _ = topo.addr(dst)
+        sent[0] += len(engs)
+        prev["g"] = add("g", lambda q: q.remote_dma(out, in_, T.sem[sem], T.sem.ls, pid, rid, bits(engs)), (0.3, "c", 0), deps, after, kind="r")
+        return prev["g"]
+
+    def LAND(i, sem, got, lat=None, at=None):
+        return add(None, None, (0.0, "c", 0), [i], kind="a", lat=lat, sem=sem, val=got, at=at)
+
+    def SEND(dst, out, in_, sem, deps, lat=None, after=()):
+        engs = topo.engines(core, dst)
+        return LAND(WRITE(dst, out, in_, sem, deps, engs, after), sem, len(engs), lat)
+
+    def rc(k):
+        return T.cores[(rank + k) % N]
+
+    F = {e: T["FR%d" % e] for e in FOFF}
+    ldj = DMA("y", T.JI[:, 0, :], T.ju[:, :])
+    lds = DMA("y", T.ST[:, 4:36], T.st[:, :])
+    ldu = DMA("s", T.U[:, 0, :], T.qu[:, :], lat=2.3)
+    ldf = []
+    for p in range(NPC):
+        a, b = p * PW, min((p + 1) * PW, 4096)
+        one = [DMA("y" if p % 2 == 0 else "s", F[0][:, a:b], T.fr[:, a:b], lat=2.8 + 2.4 * p / (NPC - 1))]
+        if p == NPC - 1:
+            one.append(DMA("y", F[0][:, 4096:FW], T.fr[:, 3968:4096], lat=3.0))
+        ldf.append(one)
+    jrdy = {0: ldj}
+    for e in JOFF[1:]:
+        jrdy[e] = SEND(rc(-e), T.JI[:, JOFF.index(e), :], T.JI[:, 0, :], "aj%d" % e, [ldj], after=[prev.get("g")])
+    urdy = {0: ldu}
+    visits = sorted(UOFF[1:], key=DELTA.index)
+    for e in visits[:1]:
+        urdy[e] = SEND(rc(e), T.U[:, UOFF.index(e), :], T.U[:, 0, :], "au%d" % e, [ldu], lat=4.0, after=[prev.get("g")])
+    frdy = {e: [] for e in FOFF}
+    frdy[0] = ldf
+    hs, on = forwarders(T, topo, rank)
+    for p in range(NPC):
+        piece = F[0][:, p * PW:(p + 1) * PW]
+        i = WRITE(hs[p], piece, piece, "af0_%d" % p, [ldf[p]], on, [prev.get("g")])
+        for x, e in enumerate(frame_order()):
+            frdy[e].append(LAND(i, "af%d_%d" % (e, p), len(topo.engines(forwarders(T, topo, (rank + e) % N)[0][p], core)), at=x))
+    for e in visits[1:]:
+        urdy[e] = SEND(rc(e), T.U[:, UOFF.index(e), :], T.U[:, 0, :], "au%d" % e, [ldu], lat=4.0, after=[prev.get("g")])
+
+    def IOTA(out, pat, n):
+        return add("g", lambda q: q.iota(out, pat, 0, -1, allow_small_or_imprecise_dtypes=True), (0.13, "c", 2 * n))
+
+    def SET(ap, val, n, deps=()):
+        return V(lambda q: q.memset(ap, val), n, deps)
+
+    def EQ(out, a, val, mul, deps):
+        return V(lambda q: q.tensor_scalar(out, a, float(val), float(mul), ALU.is_equal, ALU.mult), 128, deps)
+
+    ia = IOTA(T.A[:, 0, :], [[1, 128]], 128)
+    ib = IOTA(T.A[:, 1, :], [[1, 128]], 128)
+    ic = IOTA(T.A[:, 2, :], [[16, 8], [200, 16]], 128)
+    ie = IOTA(T.E[:, 0, :], [[16, 8]], 8)
+    ib2 = SET(T.A[:, 1, 0::16], 999.0, 8, [ib])
+    hI, hIn, hS, hW, hI32 = [T.WH[:, k, :] for k in range(5)]
+    bI, bIn, bq, bqn = [T.WB[:, k, :] for k in range(4)]
+    fI, fIn = T.WF[:, 0, :], T.WF[:, 1, :]
+    A0, A1, A2 = T.A[:, 0, :], T.A[:, 1, :], T.A[:, 2, :]
+    w = {}
+    for name, ap, src, val, mul, dep in [("hS", hS, A1, 1, 1, ib2), ("hW", hW, A2, -15, 1, ic), ("hI32", hI32, A0, 0, 1 / 32, ia),
+                                         ("bI", bI, A0, 0, 1, ia), ("bIn", bIn, A0, 0, -1, ia), ("bq", bq, A0, 0, 1 / 128, ia),
+                                         ("bqn", bqn, A0, 0, -1 / 128, ia), ("hI", hI, A0, 0, 1, ia), ("hIn", hIn, A0, 0, -1, ia),
+                                         ("fI", fI, A0, 0, 1, ia), ("fIn", fIn, A0, 0, -1, ia)]:
+        w[name] = EQ(ap, src, val, mul, [dep])
+    z0 = SET(T.Z[:, :], 0.0, 72)
+    e1 = S(lambda q: q.activation(T.E[:, 1, :], T.E[:, 0, :], ACT.Abs, bias=7.5), 8, [ie])
+    zr = V(lambda q: q.tensor_scalar(T.Z[:, 15:143:16], T.E[:, 1, :], 8.0, None, ALU.is_lt), 8, [z0, e1])
+    e2 = V(lambda q: q.tensor_scalar(T.E[:, 2, :], T.E[:, 0, :], 0.0, BIG, ALU.is_equal, ALU.mult), 8, [ie])
+    e3 = V(lambda q: q.tensor_reduce(T.E[:, 3, 0:1], T.E[:, 2, :], AxisListType.X, ALU.add), 8, [e2])
+    kc, rs = {}, {}
+    for ns, KC, RS in [(4, T.KC4, T.RS4), (6, T.KC6, T.RS6)]:
+        k0 = SET(KC[:, :], 0.0, 16 * ns)
+        kc[ns] = [SET(KC[:, 1:2 * ns:ns], BIG, 2, [k0]),
+                  V(lambda q, KC=KC, ns=ns: q.tensor_scalar(KC[:, 2::2 * ns], KC[:, 3::2 * ns], T.E[:, 3, 0:1], None, ALU.add), 16, [k0, e3])]
+        rs[ns] = SET(RS[:, 0::ns], 4 * BIG, 32, [SET(RS[:, :], 0.0, 32 * ns)])
+    sqz = {4: None, 6: [SET(T.SQ6[:, a:a + 8, 64:96], 0.0, 128) for a in range(0, 32, 8)]}
+    sc = [SET(T.SC[:, 0, :], 128.0, 16), SET(T.SC[:, 1, :], 1.0, 16), SET(T.SC[:, 2, :], -60.0, 16)]
+    rh = SET(T.R[:, :, 0:8], 0.0, 48)
+    c4 = [SET(T.C4[:, k::4], v, 32) for k, v in enumerate([-18560.0, 18560.0, 0.0, 2048.0])]
+    fn_ = [float((rank + s) % N) for s in range(N)]
+    c60 = SET(T.C6[:, :, :], 0.0, 192)
+    c6 = [SET(T.C6[:, a, k::6], v, 32, [c60]) for a, k, v in
+          [(0, 0, -18560.0), (0, 1, 18560.0), (0, 4, 2048.0), (1, 3, fn_[5] - fn_[4]), (1, 4, fn_[4])]]
+    f4 = [SET(T.F4[:, k::4], v, 32) for k, v in enumerate([fn_[3] - fn_[2], fn_[2] - fn_[1], fn_[1] - fn_[0], fn_[0]])]
+
+    def tile(s, k):
+        return (s * NCH + k) * TW
+
+    s0 = SET(T.ST[:, 0:4], 0, 4)
+    t0 = V(lambda q: q.tensor_tensor(T.T0[:, 0, :], T.ST[:, 4:36], T.JI[:, 0, :], ALU.add), 64, [lds, ldj])
+    have = {}
+    for k, (c0, c1) in enumerate(CH):
+        n, o = c1 - c0, tile(0, k)
+        have[(0, k)] = [V(lambda q, n=n, o=o, c0=c0: q.tensor_copy(T.OFF[:, o:o + n + 2], T.ST[:, c0 + 2:c0 + n + 4]), n, [s0, lds]),
+                        V(lambda q, n=n, o=o, c0=c0: q.tensor_scalar(T.OFF[:, o + n + 2:o + 2 * n + 2], T.T0[:, 0, c0:c0 + n], 0.0, 4095.0,
+                                                                     ALU.max, ALU.min), n, [t0])]
+    bank = {}
+    red_last = {}
+    hist = {}
+
+    def pick(out, x, n, deps):
+        return S(lambda q: q.activation(out, x, ACT.Identity), n, deps)
+
+    def step(s, k, scan_up, pre):
+        tag[0] = k
+        c0, c1 = CH[k]
+        n, o = c1 - c0, tile(s, k)
+        last = s == N - 1
+        ns = 6 if last else 4
+        SQ, KC, RS = (T.SQ6, T.KC6, T.RS6) if last else (T.SQ4, T.KC4, T.RS4)
+        fe = (s - DELTA[s]) % N
+        Fr, Uq = F[fe], T.U[:, UOFF.index(DELTA[s]), 16 * c0:16 * c1]
+        src = [have[(s, k)], frdy[fe], urdy[DELTA[s]]]
+        bk, bs, bu, bd = 1 + k, 3 + k, 5 + k, 7 * k
+        BK, BS, BU, BD = T["B%d" % bk], T["B%d" % bs], T["B%d" % bu], T["B%d" % bd]
+        D = [T.D[:, (s * 4 + j) * 512 + 16 * c0:(s * 4 + j) * 512 + 16 * c1] for j in range(4)]
+        P0, P1, P2, P3 = T.PH[:, o + 2:o + n + 2], T.PH[:, o + 1:o + n + 1], T.PH[:, o:o + n], T.PH[:, o + n + 2:o + 2 * n + 2]
+        fo = s * 96 + 3 * c0
+        Y0, Y1, Fd = T.FL[:, fo:fo + n], T.FL[:, fo + n:fo + 2 * n], T.FL[:, fo + 2 * n:fo + 3 * n]
+        O1, PC = T.O1[:, s * 32 + c0:s * 32 + c1], T.P1H[:, s * 32 + c0:s * 32 + c1]
+
+        def gather(j, win, off, deps):
+            return V(lambda q: q.tensor_tensor(D[j], win.indirect(off), Uq, ALU.subtract), 16 * n, [src, deps], True)
+
+        def square(j, x, deps):
+            return S(lambda q: q.activation(SQ[:, c0:c1, 16 * j:16 * j + 16], x, ACT.Square), 16 * n, [deps, red_last.get((ns, k))])
+
+        cvt = V(lambda q: q.tensor_scalar(T.PH[:, o:o + 2 * n + 2], T.OFF[:, o:o + 2 * n + 2], -2048.0, None, ALU.add), n, [have[(s, k)]])
+        stk = MM([(BS[:, 0:3 * n], bI, T.SC[:, :, 0:n], True, False), (BS[:, 0:n], hS, P0, False, False), (BS[:, 0:n], hW, P1, False, False),
+                  (BS[:, n:2 * n], hS, P0, False, False), (BS[:, n:2 * n], hW, P1, False, False), (BS[:, 2 * n:3 * n], hI32, P2, False, True)],
+                 [cvt, sc, w["bI"], w["hS"], w["hW"], w["hI32"], bank.get(bs)])
+        rnd = S(lambda q: q.activation(T.FL[:, fo:fo + 3 * n], BS[:, 0:3 * n], ACT.Identity, bias=18496.015625), 3 * n, [stk])
+        C1 = BS[:, 128:128 + n]
+        mc1 = MM([(C1, hS, P0, True, False), (C1, hW, P1, False, False), (C1, bqn, Y1, False, False), (C1, bq, Y0, False, True)],
+                 [rnd, w["bq"], w["bqn"]])
+        o1 = V(lambda q: q.tensor_scalar(O1, C1, 2048.0, None, ALU.add), n, [mc1])
+        pc = V(lambda q: q.tensor_copy(PC, C1), n, [mc1])
+        bank[bs] = [o1, pc]
+        g0 = gather(3, Fr[:, 0:4096], T.OFF[:, o + 2:o + n + 2], [])
+        g2 = gather(1, Fr[:, 128:FW], T.OFF[:, o:o + n], [])
+        g1 = gather(2, Fr[:, 0:4096], O1, [o1])
+        g3 = S(lambda q: q.activation(D[0], Fr[:, 0:4096].indirect(T.OFF[:, o + n + 2:o + 2 * n + 2]), ACT.Copy), 16 * n, [src], True)
+        u1 = MM([(BU[:, 0:16 * n], bIn, Uq, True, False)], [urdy[DELTA[s]], w["bIn"], bank.get(bu)])
+        u2 = MM([(BU[:, 0:16 * n], bI, D[0], False, True)], [g3, w["bI"]], [u1])
+        q3 = square(0, BU[:, 0:16 * n], [u2])
+        bank[bu] = [q3]
+        sq = [q3, square(3, D[3], [g0]), square(1, D[1], [g2]), square(2, D[2], [g1])]
+        K, DL, DF = BK[:, 0:ns * n], BD[:, 192:192 + ns * n], BD[:, 320:320 + ns * n]
+
+        def sl(base, j):
+            return (BD if base else BK)[:, base + j:base + ns * n:ns]
+
+        def part(terms, deps, after, base=192, stop=False):
+            return MM([(sl(base, j), a, x, False, stop and i == len(terms) - 1) for i, (j, a, x) in enumerate(terms)], deps, after)
+
+        first = T.C6[:, 0, ns * c0:ns * c1] if last else T.C4[:, ns * c0:ns * c1]
+        d = MM([(DL, bI, first, True, False)], [c6 if last else c4, w["bI"], bank.get(bd)])
+        if last:
+            bp = T.M4[:, 2, 4 * c0 + 3:4 * c1:4]
+            d = part([(4, fIn, bp), (5, fI, bp)], [pre, w["fI"], w["fIn"]], [d])
+        d = part([(0, hI, P3), (0, hIn, P2), (1, hI, P2), (4 if last else 3, hI, P0)], [cvt, w["hI"], w["hIn"]], [d])
+        d = part([(2, hIn, P0), (0, bI, Fd), (1, bIn, Fd)], [rnd, w["bIn"]], [d])
+        d = part([(1, hIn, PC), (2, hI, PC)], [pc], [d], stop=True)
+        if last:
+            bf = T.M4[:, 3, 4 * c0 + 3:4 * c1:4]
+            d = MM([(DF, bI, T.C6[:, 1, ns * c0:ns * c1], True, False), (sl(320, 4), fIn, bf, False, False)], [], [d])
+            d = part([(5, fI, bf)], [], [d], 320, True)
+        dl = d
+        d = MM([(K, bI, KC[:, ns * c0:ns * c1], True, False)], [kc[ns], w["bI"], bank.get(bk)])
+        if last:
+            d = part([(5, fI, T.M4[:, 0, 4 * c0 + 3:4 * c1:4])], [pre, w["fI"]], [d], 0)
+            d = part([(4, fI, T.HL[:, s - 1, c0:c1])], [hist[(s - 1, k)]], [d], 0)
+        red = MM([(K, T.Z[:, 15 - r:143 - r], SQ[:, c0:c1, r::16], False, r == 15) for r in range(16)], [sq, zr, sqz[ns]], [d])
+        red_last[(ns, k)] = red
+        M, NE = T.M[:, s, ns * c0:ns * c1], T.NE[:, s, ns * c0:ns * c1]
+        R = T.R[:, s, 8 + ns * c0:8 + ns * c1]
+        m1 = V(lambda q: q.tensor_tensor_scan(M, RS[:, ns * c0:ns * c1], K, 0.0, ALU.max, ALU.min), ns * n, [red, rs[ns]])
+        ne = V(lambda q: q.tensor_tensor(NE, K, M, ALU.not_equal), ns * n, [m1])
+        m2 = V(lambda q: q.tensor_tensor_scan(R, NE, DL, 0.0, ALU.mult, ALU.add), ns * n, [ne, dl])
+        bank[bk] = [ne]
+        bank[bd] = [m2]
+        if last:
+            m3 = V(lambda q: q.tensor_tensor_scan(T.RF[:, ns * c0:ns * c1], NE, DF, 0.0, ALU.mult, ALU.add), ns * n, [ne, dl])
+            yc = pick(T.Y[:, 0, c0:c1], T.M[:, s, ns * c0 + 5:ns * c1:ns], n, [m1])
+            yp = pick(T.Y[:, 2, c0:c1], T.R[:, s, 8 + ns * c0 + 5:8 + ns * c1:ns], n, [m2])
+            yf = V(lambda q: q.tensor_copy(T.Y[:, 1, c0:c1], T.RF[:, ns * c0 + 5:ns * c1:ns]), n, [m3])
+            DMA("y", T.yc[:, c0:c1], T.Y[:, 0, c0:c1], [yc])
+            DMA("s", T.yp[:, c0:c1], T.Y[:, 2, c0:c1], [yp])
+            DMA("y", T.yf[:, c0:c1], T.Y[:, 1, c0:c1], [yf])
+            return m2
+        hop = (DELTA[s + 1] - DELTA[s]) % N
+        je = (s + 1 - DELTA[s]) % N
+        X, o2 = (T.OFS if hop else T.OFF), tile(s + 1, k)
+        TJ = T.T0[:, s + 1, c0:c1]
+        xj = V(lambda q: q.tensor_tensor(TJ, T.R[:, s, 4 * c0 + 11:4 * c1 + 8:4], T.JI[:, JOFF.index(je), c0:c1], ALU.add), 2 * n, [m2, jrdy[je]])
+        x1 = V(lambda q: q.tensor_copy(X[:, o2:o2 + n + 2], T.R[:, s, 4 * c0 + 3:4 * c1 + 8:4]), n, [m2, scan_up, rh])
+        x2 = V(lambda q: q.tensor_scalar(X[:, o2 + n + 2:o2 + 2 * n + 2], TJ, 0.0, 4095.0, ALU.max, ALU.min), n, [xj])
+        if hop:
+            have[(s + 1, k)] = [SEND(rc(hop), T.OFF[:, o2:o2 + 2 * n + 2], T.OFS[:, o2:o2 + 2 * n + 2], "ao%d_%d" % (s + 1, k), [x1, x2])]
+        else:
+            have[(s + 1, k)] = [x1, x2]
+        if s == N - 2:
+            H = T.HS if DELTA[s] else T.HL
+            hh = pick(H[:, s, c0:c1], T.M[:, s, 4 * c0 + 3:4 * c1:4], n, [m1])
+            hist[(s, k)] = SEND(rc(-DELTA[s]), T.HL[:, s, c0:c1], T.HS[:, s, c0:c1], "ah%d_%d" % (s, k), [hh]) if DELTA[s] else hh
+        return m2
+
+    pre = None
+    old = []
+    for s in range(N):
+        if s == N - 1:
+            B0 = T.B0
+            lst = [(B0[:, 128 + j:256:4], fI, T.HL[:, 3 - j, 32:64], j == 0, False) for j in range(4)]
+            lst += [(B0[:, 128 + j:256:4], fIn, T.HL[:, 2 - j, 32:64], False, j == 2) for j in range(3)]
+            lst += [(B0[:, j:128:4], fI, T.HL[:, 3 - j, 0:32], j == 0, j == 3) for j in range(4)]
+            pm = MM(lst[0:1], [old, w["fI"], w["fIn"], bank.get(0)])
+            for one in lst[1:]:
+                pm = MM([one], [], [pm])
+            p1 = V(lambda q: q.tensor_tensor_scan(T.M4[:, 0, :], T.RS4[:, :], B0[:, 0:128], 0.0, ALU.max, ALU.min), 128, [pm, rs[4]])
+            p2 = V(lambda q: q.tensor_tensor(T.M4[:, 1, :], B0[:, 0:128], T.M4[:, 0, :], ALU.not_equal), 128, [p1])
+            pre = [V(lambda q: q.tensor_tensor_scan(T.M4[:, 2, :], T.M4[:, 1, :], B0[:, 128:256], 0.0, ALU.mult, ALU.add), 128, [p2]),
+                   V(lambda q: q.tensor_tensor_scan(T.M4[:, 3, :], T.M4[:, 1, :], T.F4[:, :], 0.0, ALU.mult, ALU.add), 128, [p2, f4])]
+            bank[0] = pre
+        up, ups = None, []
+        for k in range(NCH):
+            up = step(s, k, up, pre)
+            ups.append(up)
+        tag[0] = None
+        if s < N - 2:
+            H = T.HS if DELTA[s] else T.HL
+            hh = [pick(H[:, s, 0:32], T.M[:, s, 3:128:4], 32, ups), pick(H[:, s, 32:64], T.R[:, s, 11:136:4], 32, ups)]
+            old.append(SEND(rc(-DELTA[s]), T.HL[:, s, :], T.HS[:, s, :], "ah%d_0" % s, hh) if DELTA[s] else hh)
+    return ops, sent[0]
+
+
+def rank_program(g, core, T, topo):
+    rank = T.rank_of(core)
+    if rank is None:
+        helper_program(g, core, T, topo)
+        return
+    ops, sent = build(g, core, T, topo, rank)
+    if "seq" not in KEPT:
+        KEPT["seq"] = improve(ops)
+    order = {}
+    for i in KEPT["seq"]:
+        order.setdefault(ops[i]["eng"], []).append(i)
+    queue = {"v": g.vector, "s": g.scalar, "t": g.tensor, "y": g.sync, "g": g}
+    needed = set(d for o in ops for d in o["deps"])
+    total = {}
+    for eng in queue:
+        cnt = 0
+        for i in order.get(eng, []):
+            if ops[i]["kind"] == "c" and i in needed:
+                cnt += 1
+                ops[i]["sem"], ops[i]["val"] = "c" + eng, cnt
+                total["c" + eng] = cnt
+    for o in ops:
+        if o["kind"] in "da":
+            total[o["sem"]] = o["val"]
+    for eng, q in queue.items():
+        seen = {}
+        for i in order.get(eng, []):
+            o = ops[i]
+            want = {}
+            for d in o["deps"]:
+                want[ops[d]["sem"]] = max(want.get(ops[d]["sem"], 0), ops[d]["val"])
+            for sem, val in want.items():
+                if seen.get(sem, 0) < val:
+                    q.wait_ge(T.sem[sem], val)
+                    seen[sem] = val
+            ins = o["fn"](q)
+            if o["kind"] == "d":
+                ins.then_inc(T.sem[o["sem"]], 16)
+            elif o["kind"] == "c" and o["sem"]:
+                ins.then_inc(T.sem[o["sem"]], 1)
+        if eng == "g":
+            total["ls"] = sent
+            for sem, val in total.items():
+                if seen.get(sem, 0) < val:
+                    q.wait_ge(T.sem[sem], val)

@@ -4,13 +4,13 @@ from concourse.mybir import AluOpType, AxisListType, ActivationFunctionType
 N = 6
 DELTA = [0, 2, 2, 4, 4, 0]
 CH = [(0, 16), (16, 32)]
-WAYS = "fnFn"
+WAYS = "fFrr"
 ROUNDS = 40000
 FW = 4224
 TW = 72
 BIG = 8192.0
-EST = {"cy": 1.0e-3, "ga": 1.56, "pe": 0.5e-3, "wake": 0.08, "hop": 2.5, "frame": 12.0, "next": 5.0}
-SPREAD = [{}, {"cy": 0.85e-3, "ga": 1.2, "pe": 0.43e-3}, {"cy": 1.2e-3, "ga": 1.9, "pe": 0.6e-3}, {"pe": 0.9e-3}, {"hop": 3.5, "wake": 0.15}]
+EST = {"cy": 0.9e-3, "ga": 1.56, "pe": 0.55e-3, "wake": 0.17, "hop": 3.0, "frame": 13.0, "next": 5.0}
+SPREAD = [{}, {"pe": 0.83e-3, "wake": 0.12}, {"wake": 0.25, "pe": 0.45e-3}, {"cy": 1.15e-3, "ga": 1.9, "wake": 0.1}]
 
 NCH = len(CH)
 NPC = len(WAYS)
@@ -20,7 +20,7 @@ JOFF = sorted(set([0] + [(s + 1 - DELTA[s]) % N for s in range(N - 1)]))
 PW = FW // NPC
 
 SCRATCH = {
-    "U": ("sbuf", [128, len(UOFF), 512], "bfloat16"),
+    "U": ("sbuf", [128, len(UOFF), 528], "bfloat16"),
     "ST": ("sbuf", [128, 36], "int32"),
     "JI": ("sbuf", [128, len(JOFF), 32], "int32"),
     "C4": ("sbuf", [128, 128], "bfloat16"),
@@ -28,11 +28,10 @@ SCRATCH = {
     "T0": ("sbuf", [128, N, 32], "float32"),
     "OFF": ("sbuf", [128, N * NCH * TW], "uint16"),
     "OFS": ("sbuf", [128, N * NCH * TW], "uint16"),
-    "O1": ("sbuf", [128, N * 32], "uint16"),
     "PH": ("sbuf", [128, N * NCH * TW], "float16"),
-    "P1H": ("sbuf", [128, N * 32], "float16"),
     "FL": ("sbuf", [128, N * 96], "bfloat16"),
     "D": ("sbuf", [128, N * 4 * 512], "bfloat16"),
+    "D1": ("sbuf", [128, N * NCH, 272], "bfloat16"),
     "SQ4": ("sbuf", [128, 32, 64], "bfloat16"),
     "SQ6": ("sbuf", [128, 32, 96], "bfloat16"),
     "M": ("sbuf", [128, N, 192], "float32"),
@@ -52,12 +51,13 @@ SCRATCH = {
     "A": ("sbuf", [128, 3, 128], "float32"),
     "E": ("sbuf", [128, 4, 8], "float32"),
     "Z": ("sbuf", [128, 144], "bfloat16"),
-    "WH": ("sbuf", [128, 5, 128], "float16"),
+    "WH": ("sbuf", [128, 8, 128], "float16"),
     "WB": ("sbuf", [128, 4, 128], "bfloat16"),
     "WF": ("sbuf", [128, 2, 128], "float32"),
 }
 for _e in FOFF:
     SCRATCH["FR%d" % _e] = ("sbuf", [128, FW], "bfloat16")
+    SCRATCH["FS%d" % _e] = ("sbuf", [128, FW], "bfloat16")
 for _b in range(8):
     SCRATCH["B%d" % _b] = ("psum", [128, 512], "float32")
 
@@ -94,8 +94,8 @@ def forwarders(T, topo, q):
     ok = [h for h in topo.cores_of(c) if T.rank_of(h) is None and all(topo.may_write(h, d) for d in dsts)]
     far = [h for h in ok if topo.die(h) != topo.die(c)]
     near = [h for h in ok if topo.die(h) == topo.die(c)]
-    hs = [{"f": far[0], "F": far[-1], "n": near[0]}[x] for x in WAYS]
-    return hs, [y for y in topo.engines(c, hs[0]) if y not in topo.engines(c, dsts[0])]
+    hs = [{"f": far[0], "F": far[-1], "n": near[0], "r": c}[x] for x in WAYS]
+    return hs, [y for y in topo.engines(c, far[0]) if y not in topo.engines(c, dsts[0])]
 
 
 def helper_program(g, core, T, topo):
@@ -120,7 +120,7 @@ def helper_program(g, core, T, topo):
 def times(o, est):
     fix, what, n = o["cost"]
     dur = fix + n * {"c": est["cy"], "g": est["cy"] * est["ga"], "p": est["pe"]}[what]
-    return dur, (est["hop"] if o["lat"] is None else o["lat"]), (est["frame"] + o["at"] * est["next"] if o["at"] is not None else 0.0)
+    return dur, (est["hop"] if o["lat"] is None else o["lat"]), (est["frame"] + o["at"] if o["at"] is not None else 0.0)
 
 
 def schedule(ops, est, lead):
@@ -297,7 +297,7 @@ def build(g, core, T, topo, rank):
     F = {e: T["FR%d" % e] for e in FOFF}
     ldj = DMA("y", T.JI[:, 0, :], T.ju[:, :])
     lds = DMA("y", T.ST[:, 4:36], T.st[:, :])
-    ldu = DMA("s", T.U[:, 0, :], T.qu[:, :], lat=2.3)
+    ldu = DMA("s", T.U[:, 0, 0:512], T.qu[:, :], lat=2.3)
     ldf = []
     for p in range(NPC):
         a, b = p * PW, min((p + 1) * PW, 4096)
@@ -310,18 +310,24 @@ def build(g, core, T, topo, rank):
         jrdy[e] = SEND(rc(-e), T.JI[:, JOFF.index(e), :], T.JI[:, 0, :], "aj%d" % e, [ldj], after=[prev.get("g")])
     urdy = {0: ldu}
     visits = sorted(UOFF[1:], key=DELTA.index)
+
+    def queries(e):
+        urdy[e] = SEND(rc(e), T.U[:, UOFF.index(e), 0:512], T.U[:, 0, 0:512], "au%d" % e, [ldu], lat=4.0, after=[prev.get("g")])
+
     for e in visits[:1]:
-        urdy[e] = SEND(rc(e), T.U[:, UOFF.index(e), :], T.U[:, 0, :], "au%d" % e, [ldu], lat=4.0, after=[prev.get("g")])
+        queries(e)
     frdy = {e: [] for e in FOFF}
     frdy[0] = ldf
     hs, on = forwarders(T, topo, rank)
-    for p in range(NPC):
-        piece = F[0][:, p * PW:(p + 1) * PW]
-        i = WRITE(hs[p], piece, piece, "af0_%d" % p, [ldf[p]], on, [prev.get("g")])
-        for x, e in enumerate(frame_order()):
-            frdy[e].append(LAND(i, "af%d_%d" % (e, p), len(topo.engines(forwarders(T, topo, (rank + e) % N)[0][p], core)), at=x))
-    for e in visits[1:]:
-        urdy[e] = SEND(rc(e), T.U[:, UOFF.index(e), :], T.U[:, 0, :], "au%d" % e, [ldu], lat=4.0, after=[prev.get("g")])
+    for x, e in enumerate(frame_order()):
+        for p in range(NPC):
+            piece = F[0][:, p * PW:(p + 1) * PW]
+            if hs[p] == core:
+                WRITE(rc(-e), F[e][:, p * PW:(p + 1) * PW], piece, "af%d_%d" % (e, p), [ldf[p]], topo.engines(core, rc(-e)), [prev.get("g")])
+            elif x == 0:
+                WRITE(hs[p], piece, piece, "af0_%d" % p, [ldf[p]], on, [prev.get("g")])
+            frdy[e].append(LAND(prev["g"], "af%d_%d" % (e, p), len(topo.engines(forwarders(T, topo, (rank + e) % N)[0][p], core)),
+                                at=x * EST["next"] - 0.8 * (NPC - 1 - p)))
 
     def IOTA(out, pat, n):
         return add("g", lambda q: q.iota(out, pat, 0, -1, allow_small_or_imprecise_dtypes=True), (0.13, "c", 2 * n))
@@ -337,7 +343,7 @@ def build(g, core, T, topo, rank):
     ic = IOTA(T.A[:, 2, :], [[16, 8], [200, 16]], 128)
     ie = IOTA(T.E[:, 0, :], [[16, 8]], 8)
     ib2 = SET(T.A[:, 1, 0::16], 999.0, 8, [ib])
-    hI, hIn, hS, hW, hI32 = [T.WH[:, k, :] for k in range(5)]
+    hI, hIn, hS, hW, hI32, hSn, hWn, hSI = [T.WH[:, k, :] for k in range(8)]
     bI, bIn, bq, bqn = [T.WB[:, k, :] for k in range(4)]
     fI, fIn = T.WF[:, 0, :], T.WF[:, 1, :]
     A0, A1, A2 = T.A[:, 0, :], T.A[:, 1, :], T.A[:, 2, :]
@@ -345,8 +351,21 @@ def build(g, core, T, topo, rank):
     for name, ap, src, val, mul, dep in [("hS", hS, A1, 1, 1, ib2), ("hW", hW, A2, -15, 1, ic), ("hI32", hI32, A0, 0, 1 / 32, ia),
                                          ("bI", bI, A0, 0, 1, ia), ("bIn", bIn, A0, 0, -1, ia), ("bq", bq, A0, 0, 1 / 128, ia),
                                          ("bqn", bqn, A0, 0, -1 / 128, ia), ("hI", hI, A0, 0, 1, ia), ("hIn", hIn, A0, 0, -1, ia),
+                                         ("hSn", hSn, A1, 1, -1, ib2), ("hWn", hWn, A2, -15, -1, ic),
                                          ("fI", fI, A0, 0, 1, ia), ("fIn", fIn, A0, 0, -1, ia)]:
         w[name] = EQ(ap, src, val, mul, [dep])
+    w["hSI"] = V(lambda q: q.tensor_tensor(hSI, hS, hI, ALU.subtract), 128, [w["hS"], w["hI"]])
+    pads = [SET(T.U[:, :, 512:528], 0.0, 24), SET(T.D1[:, :, 0:1], 0.0, 12)]
+    srdy = {}
+    for e in FOFF:
+        FS, cp = T["FS%d" % e], []
+        for p in range(NPC):
+            a, b = max(p * PW, 1), (p + 1) * PW
+            if e == 0 and p < NPC - 1:
+                cp.append(S(lambda q, FS=FS, e=e, a=a, b=b: q.activation(FS[:, a - 1:b - 1], F[e][:, a:b], ACT.Copy), PW, [frdy[e][p]]))
+            else:
+                cp.append(V(lambda q, FS=FS, e=e, a=a, b=b: q.tensor_copy(FS[:, a - 1:b - 1], F[e][:, a:b]), PW // 2, [frdy[e][p]]))
+        srdy[e] = V(lambda q, FS=FS, e=e: q.tensor_copy(FS[:, 127:4096:128], F[e][:, 127:4096:128]), 32, [cp, frdy[e]])
     z0 = SET(T.Z[:, :], 0.0, 72)
     e1 = S(lambda q: q.activation(T.E[:, 1, :], T.E[:, 0, :], ACT.Abs, bias=7.5), 8, [ie])
     zr = V(lambda q: q.tensor_scalar(T.Z[:, 15:143:16], T.E[:, 1, :], 8.0, None, ALU.is_lt), 8, [z0, e1])
@@ -393,38 +412,35 @@ def build(g, core, T, topo, rank):
         last = s == N - 1
         ns = 6 if last else 4
         SQ, KC, RS = (T.SQ6, T.KC6, T.RS6) if last else (T.SQ4, T.KC4, T.RS4)
-        fe = (s - DELTA[s]) % N
-        Fr, Uq = F[fe], T.U[:, UOFF.index(DELTA[s]), 16 * c0:16 * c1]
-        src = [have[(s, k)], frdy[fe], urdy[DELTA[s]]]
+        fe, ui = (s - DELTA[s]) % N, UOFF.index(DELTA[s])
+        Fr, Uq = F[fe], T.U[:, ui, 16 * c0:16 * c1]
+        lists = have[(s, k)]
+        own, jumped = (lists[0], lists[1]) if len(lists) == 2 else (lists, lists)
         bk, bs, bu, bd = 1 + k, 3 + k, 5 + k, 7 * k
         BK, BS, BU, BD = T["B%d" % bk], T["B%d" % bs], T["B%d" % bu], T["B%d" % bd]
         D = [T.D[:, (s * 4 + j) * 512 + 16 * c0:(s * 4 + j) * 512 + 16 * c1] for j in range(4)]
+        D[2] = T.D1[:, s * NCH + k, 0:16 * n]
         P0, P1, P2, P3 = T.PH[:, o + 2:o + n + 2], T.PH[:, o + 1:o + n + 1], T.PH[:, o:o + n], T.PH[:, o + n + 2:o + 2 * n + 2]
         fo = s * 96 + 3 * c0
         Y0, Y1, Fd = T.FL[:, fo:fo + n], T.FL[:, fo + n:fo + 2 * n], T.FL[:, fo + 2 * n:fo + 3 * n]
-        O1, PC = T.O1[:, s * 32 + c0:s * 32 + c1], T.P1H[:, s * 32 + c0:s * 32 + c1]
 
-        def gather(j, win, off, deps):
-            return V(lambda q: q.tensor_tensor(D[j], win.indirect(off), Uq, ALU.subtract), 16 * n, [src, deps], True)
+        def gather(out, win, off, u, deps):
+            return V(lambda q: q.tensor_tensor(out, win.indirect(off), u, ALU.subtract), 16 * n, [own, frdy[fe], urdy[DELTA[s]], deps], True)
 
         def square(j, x, deps):
             return S(lambda q: q.activation(SQ[:, c0:c1, 16 * j:16 * j + 16], x, ACT.Square), 16 * n, [deps, red_last.get((ns, k))])
 
-        cvt = V(lambda q: q.tensor_scalar(T.PH[:, o:o + 2 * n + 2], T.OFF[:, o:o + 2 * n + 2], -2048.0, None, ALU.add), n, [have[(s, k)]])
+        cvt = V(lambda q: q.tensor_scalar(T.PH[:, o:o + 2 * n + 2], T.OFF[:, o:o + 2 * n + 2], -2048.0, None, ALU.add), n, [lists])
         stk = MM([(BS[:, 0:3 * n], bI, T.SC[:, :, 0:n], True, False), (BS[:, 0:n], hS, P0, False, False), (BS[:, 0:n], hW, P1, False, False),
                   (BS[:, n:2 * n], hS, P0, False, False), (BS[:, n:2 * n], hW, P1, False, False), (BS[:, 2 * n:3 * n], hI32, P2, False, True)],
                  [cvt, sc, w["bI"], w["hS"], w["hW"], w["hI32"], bank.get(bs)])
         rnd = S(lambda q: q.activation(T.FL[:, fo:fo + 3 * n], BS[:, 0:3 * n], ACT.Identity, bias=18496.015625), 3 * n, [stk])
-        C1 = BS[:, 128:128 + n]
-        mc1 = MM([(C1, hS, P0, True, False), (C1, hW, P1, False, False), (C1, bqn, Y1, False, False), (C1, bq, Y0, False, True)],
-                 [rnd, w["bq"], w["bqn"]])
-        o1 = V(lambda q: q.tensor_scalar(O1, C1, 2048.0, None, ALU.add), n, [mc1])
-        pc = V(lambda q: q.tensor_copy(PC, C1), n, [mc1])
-        bank[bs] = [o1, pc]
-        g0 = gather(3, Fr[:, 0:4096], T.OFF[:, o + 2:o + n + 2], [])
-        g2 = gather(1, Fr[:, 128:FW], T.OFF[:, o:o + n], [])
-        g1 = gather(2, Fr[:, 0:4096], O1, [o1])
-        g3 = S(lambda q: q.activation(D[0], Fr[:, 0:4096].indirect(T.OFF[:, o + n + 2:o + 2 * n + 2]), ACT.Copy), 16 * n, [src], True)
+        bank[bs] = [rnd]
+        g0 = gather(D[3], Fr[:, 0:4096], T.OFF[:, o + 2:o + n + 2], Uq, [])
+        g2 = gather(D[1], Fr[:, 128:FW], T.OFF[:, o:o + n], Uq, [])
+        g1 = gather(T.D1[:, s * NCH + k, 1:16 * n + 1], T["FS%d" % fe][:, 0:4096], T.OFF[:, o + 2:o + n + 2],
+                    T.U[:, ui, 16 * c0 + 1:16 * c1 + 1], [srdy[fe], pads])
+        g3 = S(lambda q: q.activation(D[0], Fr[:, 0:4096].indirect(T.OFF[:, o + n + 2:o + 2 * n + 2]), ACT.Copy), 16 * n, [jumped, frdy[fe]], True)
         u1 = MM([(BU[:, 0:16 * n], bIn, Uq, True, False)], [urdy[DELTA[s]], w["bIn"], bank.get(bu)])
         u2 = MM([(BU[:, 0:16 * n], bI, D[0], False, True)], [g3, w["bI"]], [u1])
         q3 = square(0, BU[:, 0:16 * n], [u2])
@@ -444,8 +460,9 @@ def build(g, core, T, topo, rank):
             bp = T.M4[:, 2, 4 * c0 + 3:4 * c1:4]
             d = part([(4, fIn, bp), (5, fI, bp)], [pre, w["fI"], w["fIn"]], [d])
         d = part([(0, hI, P3), (0, hIn, P2), (1, hI, P2), (4 if last else 3, hI, P0)], [cvt, w["hI"], w["hIn"]], [d])
-        d = part([(2, hIn, P0), (0, bI, Fd), (1, bIn, Fd)], [rnd, w["bIn"]], [d])
-        d = part([(1, hIn, PC), (2, hI, PC)], [pc], [d], stop=True)
+        d = part([(1, hSn, P0), (1, hWn, P1), (2, hSI, P0), (2, hW, P1)], [w["hSn"], w["hWn"], w["hSI"], w["hW"]], [d])
+        d = part([(0, bI, Fd), (1, bIn, Fd), (1, bq, Y1)], [rnd, w["bIn"], w["bq"], w["bqn"]], [d])
+        d = part([(1, bqn, Y0), (2, bqn, Y1), (2, bq, Y0)], [], [d], stop=True)
         if last:
             bf = T.M4[:, 3, 4 * c0 + 3:4 * c1:4]
             d = MM([(DF, bI, T.C6[:, 1, ns * c0:ns * c1], True, False), (sl(320, 4), fIn, bf, False, False)], [], [d])
@@ -511,6 +528,9 @@ def build(g, core, T, topo, rank):
             up = step(s, k, up, pre)
             ups.append(up)
         tag[0] = None
+        if s == 0:
+            for e in visits[1:]:
+                queries(e)
         if s < N - 2:
             H = T.HS if DELTA[s] else T.HL
             hh = [pick(H[:, s, 0:32], T.M[:, s, 3:128:4], 32, ups), pick(H[:, s, 32:64], T.R[:, s, 11:136:4], 32, ups)]

@@ -2,15 +2,22 @@ import math
 from concourse.mybir import AluOpType, AxisListType, ActivationFunctionType
 
 N = 6
-DELTA = [0, 2, 2, 4, 4, 0]
+DELTA = [0, 1, 1, 3, 3, 0]
 CH = [(0, 16), (16, 32)]
-WAYS = "fFrr"
-ROUNDS = 40000
+WAYS = "ffrr"
+LATE = "ffFF"
+HELD = 0
+HALF = -129 / 256
+HALVES = "ssssssssssss"
+RIGHT = "ssssssssssss"
+JUMPED = "ssssssssssss"
+PASSES = 600
+ROUNDS = 30000
 FW = 4224
-TW = 72
+TW = 128
 BIG = 8192.0
-EST = {"cy": 0.9e-3, "ga": 1.56, "pe": 0.55e-3, "wake": 0.17, "hop": 3.0, "frame": 13.0, "next": 5.0}
-SPREAD = [{}, {"pe": 0.83e-3, "wake": 0.12}, {"wake": 0.25, "pe": 0.45e-3}, {"cy": 1.15e-3, "ga": 1.9, "wake": 0.1}]
+EST = {"cy": 0.9e-3, "ga": 1.56, "pe": 0.5e-3, "wake": 0.13, "hop": 2.4, "frame": 14.5, "next": 10.0}
+SPREAD = [{}, {"pe": 0.7e-3, "wake": 0.1, "hop": 2.0, "frame": 13.0}, {"wake": 0.2, "pe": 0.45e-3, "hop": 3.0, "frame": 16.0}, {"cy": 1.15e-3, "ga": 1.9, "wake": 0.1}]
 
 NCH = len(CH)
 NPC = len(WAYS)
@@ -22,50 +29,51 @@ PW = FW // NPC
 SCRATCH = {
     "U": ("sbuf", [128, len(UOFF), 528], "bfloat16"),
     "ST": ("sbuf", [128, 36], "int32"),
-    "JI": ("sbuf", [128, len(JOFF), 32], "int32"),
-    "C4": ("sbuf", [128, 128], "bfloat16"),
-    "C6": ("sbuf", [128, 2, 192], "bfloat16"),
-    "T0": ("sbuf", [128, N, 32], "float32"),
+    "JI": ("sbuf", [128, 32], "int32"),
+    "JF": ("sbuf", [128, len(JOFF), 64], "bfloat16"),
+    "C5": ("sbuf", [128, 160], "bfloat16"),
+    "C7": ("sbuf", [128, 2, 224], "bfloat16"),
+    "T0": ("sbuf", [128, 3, 36], "float32"),
     "OFF": ("sbuf", [128, N * NCH * TW], "uint16"),
     "OFS": ("sbuf", [128, N * NCH * TW], "uint16"),
     "PH": ("sbuf", [128, N * NCH * TW], "float16"),
-    "FL": ("sbuf", [128, N * 96], "bfloat16"),
+    "FL": ("sbuf", [128, N * NCH * TW], "bfloat16"),
     "D": ("sbuf", [128, N * 4 * 512], "bfloat16"),
-    "D1": ("sbuf", [128, N * NCH, 272], "bfloat16"),
-    "SQ4": ("sbuf", [128, 32, 64], "bfloat16"),
-    "SQ6": ("sbuf", [128, 32, 96], "bfloat16"),
-    "M": ("sbuf", [128, N, 192], "float32"),
-    "NE": ("sbuf", [128, N, 192], "float32"),
-    "R": ("sbuf", [128, N, 208], "float32"),
-    "RF": ("sbuf", [128, 192], "float32"),
-    "M4": ("sbuf", [128, 4, 128], "float32"),
-    "F4": ("sbuf", [128, 128], "float32"),
-    "RS4": ("sbuf", [128, 128], "float32"),
-    "RS6": ("sbuf", [128, 192], "float32"),
-    "KC4": ("sbuf", [128, 128], "bfloat16"),
-    "KC6": ("sbuf", [128, 192], "bfloat16"),
-    "SC": ("sbuf", [128, 3, 32], "bfloat16"),
-    "HS": ("sbuf", [128, N, 64], "float32"),
-    "HL": ("sbuf", [128, N, 64], "float32"),
+    "D1": ("sbuf", [128, N * NCH, 336], "bfloat16"),
+    "SQ": ("sbuf", [128, 32, 112], "bfloat16"),
+    "M": ("sbuf", [128, N, 224], "float32"),
+    "NE": ("sbuf", [128, N, 224], "float32"),
+    "RS5": ("sbuf", [128, 160], "float32"),
+    "R": ("sbuf", [128, N, 240], "float32"),
+    "RF": ("sbuf", [128, 224], "float32"),
+    "M3": ("sbuf", [128, 4, 96], "float16"),
+    "F3": ("sbuf", [128, 96], "float32"),
+    "RS3": ("sbuf", [128, 96], "float32"),
+    "RS7": ("sbuf", [128, 224], "float32"),
+    "KC5": ("sbuf", [128, 160], "bfloat16"),
+    "KC7": ("sbuf", [128, 224], "bfloat16"),
+    "SC": ("sbuf", [128, 136], "bfloat16"),
+    "HS": ("sbuf", [128, N, 256], "uint16"),
+    "HL": ("sbuf", [128, N, 256], "uint16"),
+    "HH": ("sbuf", [128, N, 256], "float16"),
     "Y": ("sbuf", [128, 3, 32], "float32"),
     "A": ("sbuf", [128, 3, 128], "float32"),
     "E": ("sbuf", [128, 4, 8], "float32"),
     "Z": ("sbuf", [128, 144], "bfloat16"),
-    "WH": ("sbuf", [128, 8, 128], "float16"),
-    "WB": ("sbuf", [128, 4, 128], "bfloat16"),
-    "WF": ("sbuf", [128, 2, 128], "float32"),
+    "WH": ("sbuf", [128, 13, 128], "float16"),
+    "SX": ("sbuf", [128, 36], "int32"),
+    "WB": ("sbuf", [128, 8, 128], "bfloat16"),
 }
 for _e in FOFF:
     SCRATCH["FR%d" % _e] = ("sbuf", [128, FW], "bfloat16")
-    SCRATCH["FS%d" % _e] = ("sbuf", [128, FW], "bfloat16")
 for _b in range(8):
     SCRATCH["B%d" % _b] = ("psum", [128, 512], "float32")
 
-SEMAPHORES = (["cv", "cs", "ct", "cg", "ls"] + ["d%d" % i for i in range(24)]
+SEMAPHORES = (["cv", "cs", "ct", "cg", "ls"] + ["d%d" % i for i in range(40)]
               + ["ao%d_%d" % (s, k) for s in range(N) for k in range(NCH)]
-              + ["ah%d_%d" % (s, k) for s in range(N) for k in range(NCH)]
+              + ["ah%d" % s for s in range(N)]
               + ["au%d" % e for e in UOFF] + ["aj%d" % e for e in JOFF]
-              + ["af%d_%d" % (e, p) for e in FOFF for p in range(NPC)])
+              + ["af%d_%d" % (e, p) for e in FOFF for p in range(NPC)] + ["al%d" % p for p in range(NPC)])
 
 ALU = AluOpType
 ACT = ActivationFunctionType
@@ -88,14 +96,34 @@ def frame_order():
     return out
 
 
+def runs(keys):
+    out = []
+    for p, x in enumerate(keys):
+        if out and out[-1][2] == x:
+            out[-1] = (out[-1][0], p + 1, x)
+        else:
+            out.append((p, p + 1, x))
+    return out
+
+
 def forwarders(T, topo, q):
     c = T.cores[q]
     dsts = [T.cores[(q - e) % N] for e in frame_order()]
     ok = [h for h in topo.cores_of(c) if T.rank_of(h) is None and all(topo.may_write(h, d) for d in dsts)]
     far = [h for h in ok if topo.die(h) != topo.die(c)]
     near = [h for h in ok if topo.die(h) == topo.die(c)]
-    hs = [{"f": far[0], "F": far[-1], "n": near[0], "r": c}[x] for x in WAYS]
-    return hs, [y for y in topo.engines(c, far[0]) if y not in topo.engines(c, dsts[0])]
+    on = [y for y in topo.engines(c, far[0]) if "r" not in WAYS or y not in topo.engines(c, dsts[0])]
+    return {"f": far[0], "F": far[-1], "n": near[0], "r": c}, on
+
+
+def again():
+    if len(frame_order()) < 2:
+        return []
+    return [x for x in runs([b if a != b else None for a, b in zip(WAYS, LATE)]) if x[2] is not None]
+
+
+def sends(x):
+    return runs(LATE) if x else [(p, p + 1, WAYS[p]) for p in range(NPC)]
 
 
 def helper_program(g, core, T, topo):
@@ -105,12 +133,16 @@ def helper_program(g, core, T, topo):
         for x, e in enumerate(frame_order()):
             dst = T.cores[(q - e) % N]
             rid, pid, _ = topo.addr(dst)
-            for p in range(NPC):
-                if hs[p] != core:
+            for a, b, who in sends(x):
+                if hs[who] != core:
                     continue
                 if x == 0:
-                    g.wait_ge(T.sem["af0_%d" % p], len(on))
-                g.remote_dma(T["FR%d" % e][:, p * PW:(p + 1) * PW], T.FR0[:, p * PW:(p + 1) * PW], T.sem["af%d_%d" % (e, p)],
+                    g.wait_ge(T.sem["af0_%d" % a], len(on))
+                if x == 1:
+                    for a2, b2, who2 in again():
+                        if hs[who2] == core and a2 < b and a < b2:
+                            g.wait_ge(T.sem["al%d" % a2], len(on))
+                g.remote_dma(T["FR%d" % e][:, a * PW:b * PW], T.FR0[:, a * PW:b * PW], T.sem["af%d_%d" % (e, a)],
                              T.sem.ls, pid, rid, topo.mask(core, dst))
                 sent += len(topo.engines(core, dst))
     if sent:
@@ -123,45 +155,55 @@ def times(o, est):
     return dur, (est["hop"] if o["lat"] is None else o["lat"]), (est["frame"] + o["at"] if o["at"] is not None else 0.0)
 
 
-def schedule(ops, est, lead):
+def place(order, before, eng, dur, early):
+    st, busy = [0.0] * len(eng), {}
+    for i in order:
+        t = early[i]
+        for j, gap in before[i]:
+            if st[j] + gap > t:
+                t = st[j] + gap
+        if eng[i]:
+            b = busy.setdefault(eng[i], [])
+            k = len(b)
+            while k and b[k - 1][1] > t:
+                k -= 1
+            while k < len(b) and b[k][0] < t + dur[i] - 1e-9:
+                t = max(t, b[k][1])
+                k += 1
+            b.insert(k, (t, t + dur[i]))
+        st[i] = t
+    return st
+
+
+def schedule(ops, est, rnd):
     n = len(ops)
-    wake = est["wake"]
     tm = [times(o, est) for o in ops]
-    succ = [[] for _ in range(n)]
-    for i, o in enumerate(ops):
-        for d in o["deps"] + o["after"]:
-            succ[d].append(i)
-    pr = [0.0] * n
-    for i in range(n - 1, -1, -1):
-        pr[i] = tm[i][0] + tm[i][1] + max([pr[j] + wake for j in succ[i]] + [0.0])
+    eng, dur, tail = [o["eng"] for o in ops], [x[0] for x in tm], [x[1] for x in tm]
+    early = [max(0.0, x[2] - x[0] - x[1]) for x in tm]
+    fw = [[(d, dur[d] + tail[d] + est["wake"]) for d in o["deps"]] + [(d, dur[d]) for d in o["after"]] for o in ops]
+    bw = [[] for _ in ops]
     for i in range(n):
-        if ops[i]["tag"] == 0:
-            pr[i] += lead
-    left = [len(o["deps"]) + len(o["after"]) for o in ops]
-    ready = [0.0] * n
-    free = {}
-    seq = []
-    avail = [i for i in range(n) if left[i] == 0]
-    while avail:
-        best = None
-        for i in avail:
-            st = max(ready[i], free.get(ops[i]["eng"], 0.0)) if ops[i]["eng"] else ready[i]
-            if best is None or st < best[0]:
-                best = (st, ops[i]["eng"])
-        t0, eng = best
-        i = max([i for i in avail if ops[i]["eng"] == eng and ready[i] <= t0 + 0.2], key=lambda j: (pr[j], -j))
-        st = max(t0, ready[i])
-        if eng:
-            free[eng] = st + tm[i][0]
-        fin = max(st + tm[i][0] + tm[i][1], tm[i][2])
-        seq.append(i)
-        avail.remove(i)
-        for j in succ[i]:
-            ready[j] = max(ready[j], fin + wake if i in ops[j]["deps"] else st + tm[i][0])
-            left[j] -= 1
-            if left[j] == 0:
-                avail.append(j)
-    return seq
+        for d, gap in fw[i]:
+            bw[d].append((i, gap - dur[d] + dur[i]))
+
+    def turn(st, links, way):
+        key = [-(st[i] + dur[i]) + ((rnd(201) - 100) / 500 if rnd(5) == 0 else 0.0) for i in range(n)]
+        for i in range(n)[::way]:
+            for j, _ in links[i]:
+                key[i] = max(key[i], key[j])
+        return sorted(range(n), key=lambda i: (key[i], way * i))
+
+    back = place(range(n - 1, -1, -1), bw, [None] * n, dur, tail)
+    best = cur = (1e9, None)
+    for _ in range(PASSES):
+        st = place(turn(back, fw, 1), fw, eng, dur, early)
+        end = max(st[i] + dur[i] + tail[i] for i in range(n))
+        if end < cur[0] + 0.3:
+            cur = (end, st)
+        if end < best[0]:
+            best = (end, st)
+        back = place(turn(cur[1], bw, -1), bw, eng, dur, tail)
+    return sorted(range(n), key=lambda i: (round(best[1][i], 6), i))
 
 
 def play(seq, ops, tm, wake):
@@ -193,13 +235,14 @@ def improve(ops):
         return sum(play(s, ops, tm, wk)[0] for tm, wk in cases) / len(cases)
 
     pre = [set(o["deps"] + o["after"]) for o in ops]
-    cur, seq = min((cost(s), s) for s in [schedule(ops, EST, 0.25 * d) for d in range(14)])
-    best, kept = cur, seq
     x = [12345]
 
     def rnd(m):
         x[0] = (x[0] * 1103515245 + 12345) % 2147483648
         return (x[0] >> 8) % m
+
+    cur, seq = min((cost(s), s) for s in [schedule(ops, EST, rnd) for _ in range(4)])
+    best, kept = cur, seq
 
     for it in range(ROUNDS):
         if it % 300 == 0:
@@ -257,7 +300,7 @@ def build(g, core, T, topo, rank):
         return len(ops) - 1
 
     def V(fn, n, deps=(), gather=False):
-        return add("v", fn, (0.05, "g", n) if gather else (0.0, "c", max(n, 64)), deps)
+        return add("v", fn, (0.05, "g", n) if gather else (0.01, "c", max(n, 64)), deps)
 
     def S(fn, n, deps=(), gather=False):
         return add("s", fn, (0.065, "g", n) if gather else (0.03, "c", max(n, 64)), deps)
@@ -295,7 +338,7 @@ def build(g, core, T, topo, rank):
         return T.cores[(rank + k) % N]
 
     F = {e: T["FR%d" % e] for e in FOFF}
-    ldj = DMA("y", T.JI[:, 0, :], T.ju[:, :])
+    ldj = DMA("y", T.JI[:, :], T.ju[:, :])
     lds = DMA("y", T.ST[:, 4:36], T.st[:, :])
     ldu = DMA("s", T.U[:, 0, 0:512], T.qu[:, :], lat=2.3)
     ldf = []
@@ -305,29 +348,42 @@ def build(g, core, T, topo, rank):
         if p == NPC - 1:
             one.append(DMA("y", F[0][:, 4096:FW], T.fr[:, 3968:4096], lat=3.0))
         ldf.append(one)
-    jrdy = {0: ldj}
-    for e in JOFF[1:]:
-        jrdy[e] = SEND(rc(-e), T.JI[:, JOFF.index(e), :], T.JI[:, 0, :], "aj%d" % e, [ldj], after=[prev.get("g")])
+    jh = V(lambda q: q.tensor_copy(T.JF[:, 0, 0:32], T.JI[:, :]), 32, [ldj])
+    jrdy = {0: V(lambda q: q.tensor_tensor(T.JF[:, 0, 32:64], T.JI[:, :], T.JF[:, 0, 0:32], ALU.subtract), 64, [jh])}
     urdy = {0: ldu}
     visits = sorted(UOFF[1:], key=DELTA.index)
+    jorder = sorted(JOFF[1:], key=[(s + 1 - DELTA[s]) % N for s in range(N - 1)].index)
 
-    def queries(e):
-        urdy[e] = SEND(rc(e), T.U[:, UOFF.index(e), 0:512], T.U[:, 0, 0:512], "au%d" % e, [ldu], lat=4.0, after=[prev.get("g")])
+    def jumps(e, after):
+        jrdy[e] = SEND(rc(-e), T.JF[:, JOFF.index(e), :], T.JF[:, 0, :], "aj%d" % e, [jrdy[0]], lat=4.0, after=after)
 
-    for e in visits[:1]:
-        queries(e)
+    def queries(e, after):
+        urdy[e] = SEND(rc(e), T.U[:, UOFF.index(e), 0:512], T.U[:, 0, 0:512], "au%d" % e, [ldu], lat=4.0, after=after)
+
+    jumps(jorder[0], [])
+    queries(visits[0], [prev["g"]])
     frdy = {e: [] for e in FOFF}
     frdy[0] = ldf
     hs, on = forwarders(T, topo, rank)
+
+    def direct(e, a, b):
+        frdy[e].append(SEND(rc(-e), F[e][:, a * PW:b * PW], F[0][:, a * PW:b * PW], "af%d_%d" % (e, a), ldf[a:b], lat=4.0, after=[prev["g"]]))
+
     for x, e in enumerate(frame_order()):
-        for p in range(NPC):
-            piece = F[0][:, p * PW:(p + 1) * PW]
-            if hs[p] == core:
-                WRITE(rc(-e), F[e][:, p * PW:(p + 1) * PW], piece, "af%d_%d" % (e, p), [ldf[p]], topo.engines(core, rc(-e)), [prev.get("g")])
-            elif x == 0:
-                WRITE(hs[p], piece, piece, "af0_%d" % p, [ldf[p]], on, [prev.get("g")])
-            frdy[e].append(LAND(prev["g"], "af%d_%d" % (e, p), len(topo.engines(forwarders(T, topo, (rank + e) % N)[0][p], core)),
-                                at=x * EST["next"] - 0.8 * (NPC - 1 - p)))
+        for a, b, who in (again() if x == 1 else []):
+            piece = F[0][:, a * PW:b * PW]
+            WRITE(hs[who], piece, piece, "al%d" % a, ldf[a:b], on, [prev["g"]])
+        for a, b, who in sends(x):
+            piece = F[0][:, a * PW:b * PW]
+            if hs[who] == core:
+                if a < NPC - HELD:
+                    direct(e, a, b)
+                continue
+            if x == 0:
+                WRITE(hs[who], piece, piece, "af0_%d" % a, ldf[a:b], on, [prev["g"]])
+            frdy[e].append(LAND(prev["g"], "af%d_%d" % (e, a), len(topo.engines(forwarders(T, topo, (rank + e) % N)[0][who], core)),
+                                at=x * EST["next"]))
+    early = prev["g"]
 
     def IOTA(out, pat, n):
         return add("g", lambda q: q.iota(out, pat, 0, -1, allow_small_or_imprecise_dtypes=True), (0.13, "c", 2 * n))
@@ -343,198 +399,229 @@ def build(g, core, T, topo, rank):
     ic = IOTA(T.A[:, 2, :], [[16, 8], [200, 16]], 128)
     ie = IOTA(T.E[:, 0, :], [[16, 8]], 8)
     ib2 = SET(T.A[:, 1, 0::16], 999.0, 8, [ib])
-    hI, hIn, hS, hW, hI32, hSn, hWn, hSI = [T.WH[:, k, :] for k in range(8)]
-    bI, bIn, bq, bqn = [T.WB[:, k, :] for k in range(4)]
-    fI, fIn = T.WF[:, 0, :], T.WF[:, 1, :]
     A0, A1, A2 = T.A[:, 0, :], T.A[:, 1, :], T.A[:, 2, :]
-    w = {}
-    for name, ap, src, val, mul, dep in [("hS", hS, A1, 1, 1, ib2), ("hW", hW, A2, -15, 1, ic), ("hI32", hI32, A0, 0, 1 / 32, ia),
-                                         ("bI", bI, A0, 0, 1, ia), ("bIn", bIn, A0, 0, -1, ia), ("bq", bq, A0, 0, 1 / 128, ia),
-                                         ("bqn", bqn, A0, 0, -1 / 128, ia), ("hI", hI, A0, 0, 1, ia), ("hIn", hIn, A0, 0, -1, ia),
-                                         ("hSn", hSn, A1, 1, -1, ib2), ("hWn", hWn, A2, -15, -1, ic),
-                                         ("fI", fI, A0, 0, 1, ia), ("fIn", fIn, A0, 0, -1, ia)]:
-        w[name] = EQ(ap, src, val, mul, [dep])
-    w["hSI"] = V(lambda q: q.tensor_tensor(hSI, hS, hI, ALU.subtract), 128, [w["hS"], w["hI"]])
+    W, w, used = {}, {}, {"h": 0, "b": 0, "f": 0}
+    al, qu = 127 / 128, 1 / 128
+    for name, mul in [("hI", 1), ("hI32", 1 / 32), ("bI", 1), ("bIn", -1), ("hIa", al), ("hIan", -al), ("hSa", al), ("hSan", -al),
+                      ("hWa", al), ("hWan", -al), ("bIq", qu), ("bIqn", -qu), ("bSqn", -qu), ("bWq", qu), ("bWqn", -qu), ("bSI", None),
+                      ("hIn", -1), ("hS", 1), ("hW", 1), ("hSn", -1), ("hWn", -1)]:
+        W[name] = {"h": T.WH, "b": T.WB}[name[0]][:, used[name[0]], :]
+        used[name[0]] += 1
+        if mul is not None:
+            src, val, dep = {"I": (A0, 0, ia), "S": (A1, 1, ib2), "W": (A2, -15, ic)}[name[1]]
+            w[name] = EQ(W[name], src, val, mul, [dep])
+    w["bSI"] = V(lambda q: q.tensor_tensor(W["bSI"], W["bIqn"], W["bSqn"], ALU.subtract), 128, [w["bIqn"], w["bSqn"]])
+    bI, bIn = W["bI"], W["bIn"]
     pads = [SET(T.U[:, :, 512:528], 0.0, 24), SET(T.D1[:, :, 0:1], 0.0, 12)]
-    srdy = {}
-    for e in FOFF:
-        FS, cp = T["FS%d" % e], []
-        for p in range(NPC):
-            a, b = max(p * PW, 1), (p + 1) * PW
-            if e == 0 and p < NPC - 1:
-                cp.append(S(lambda q, FS=FS, e=e, a=a, b=b: q.activation(FS[:, a - 1:b - 1], F[e][:, a:b], ACT.Copy), PW, [frdy[e][p]]))
-            else:
-                cp.append(V(lambda q, FS=FS, e=e, a=a, b=b: q.tensor_copy(FS[:, a - 1:b - 1], F[e][:, a:b]), PW // 2, [frdy[e][p]]))
-        srdy[e] = V(lambda q, FS=FS, e=e: q.tensor_copy(FS[:, 127:4096:128], F[e][:, 127:4096:128]), 32, [cp, frdy[e]])
     z0 = SET(T.Z[:, :], 0.0, 72)
     e1 = S(lambda q: q.activation(T.E[:, 1, :], T.E[:, 0, :], ACT.Abs, bias=7.5), 8, [ie])
     zr = V(lambda q: q.tensor_scalar(T.Z[:, 15:143:16], T.E[:, 1, :], 8.0, None, ALU.is_lt), 8, [z0, e1])
     e2 = V(lambda q: q.tensor_scalar(T.E[:, 2, :], T.E[:, 0, :], 0.0, BIG, ALU.is_equal, ALU.mult), 8, [ie])
     e3 = V(lambda q: q.tensor_reduce(T.E[:, 3, 0:1], T.E[:, 2, :], AxisListType.X, ALU.add), 8, [e2])
     kc, rs = {}, {}
-    for ns, KC, RS in [(4, T.KC4, T.RS4), (6, T.KC6, T.RS6)]:
+    for ns, KC in [(5, T.KC5), (7, T.KC7)]:
         k0 = SET(KC[:, :], 0.0, 16 * ns)
         kc[ns] = [SET(KC[:, 1:2 * ns:ns], BIG, 2, [k0]),
                   V(lambda q, KC=KC, ns=ns: q.tensor_scalar(KC[:, 2::2 * ns], KC[:, 3::2 * ns], T.E[:, 3, 0:1], None, ALU.add), 16, [k0, e3])]
-        rs[ns] = SET(RS[:, 0::ns], 4 * BIG, 32, [SET(RS[:, :], 0.0, 32 * ns)])
-    sqz = {4: None, 6: [SET(T.SQ6[:, a:a + 8, 64:96], 0.0, 128) for a in range(0, 32, 8)]}
-    sc = [SET(T.SC[:, 0, :], 128.0, 16), SET(T.SC[:, 1, :], 1.0, 16), SET(T.SC[:, 2, :], -60.0, 16)]
-    rh = SET(T.R[:, :, 0:8], 0.0, 48)
-    c4 = [SET(T.C4[:, k::4], v, 32) for k, v in enumerate([-18560.0, 18560.0, 0.0, 2048.0])]
+    kc[5].append(SET(T.KC5[:, 4::5], 2 * BIG, 32, [kc[5]]))
+    kc[7] += [SET(T.KC7[:, j::7], 2048.0, 32, [kc[7]]) for j in (4, 5, 6)]
+    for ns, RS in [(3, T.RS3), (5, T.RS5), (7, T.RS7)]:
+        rs[ns] = SET(RS[:, 0::ns], 4 * BIG, 32, [SET(RS[:, :], -BIG, 32 * ns)])
+    sqz = {5: [SET(T.SQ[:, a:a + 16, 64:80], 0.0, 128) for a in (0, 16)]}
+    sqz[7] = sqz[5] + [SET(T.SQ[:, a:a + 8, 80:112], 0.0, 128) for a in range(0, 32, 8)]
+    sc = [SET(T.SC[:, 0:32], -60.0, 16), SET(T.SC[:, 32:104], 0.5, 36)]
+    rh = SET(T.R[:, :, 0:10], 0.0, 60)
+    c50 = SET(T.C5[:, :], 0.0, 80)
+    c5 = [SET(T.C5[:, k::5], v, 32, [c50]) for k, v in [(0, -18560.0), (1, 18560.0), (3, 1904.0)]]
     fn_ = [float((rank + s) % N) for s in range(N)]
-    c60 = SET(T.C6[:, :, :], 0.0, 192)
-    c6 = [SET(T.C6[:, a, k::6], v, 32, [c60]) for a, k, v in
-          [(0, 0, -18560.0), (0, 1, 18560.0), (0, 4, 2048.0), (1, 3, fn_[5] - fn_[4]), (1, 4, fn_[4])]]
-    f4 = [SET(T.F4[:, k::4], v, 32) for k, v in enumerate([fn_[3] - fn_[2], fn_[2] - fn_[1], fn_[1] - fn_[0], fn_[0]])]
+    c70 = SET(T.C7[:, :, :], 0.0, 224)
+    c7 = [SET(T.C7[:, a, k::7], v, 32, [c70]) for a, k, v in
+          [(0, 0, -18560.0), (0, 1, 18560.0), (0, 6, 2048.0), (1, 3, fn_[5] - fn_[4]), (1, 4, fn_[4] - fn_[3]), (1, 5, fn_[3])]]
+    f3 = [SET(T.F3[:, k::3], v, 32) for k, v in enumerate([fn_[2] - fn_[1], fn_[1] - fn_[0], fn_[0]])]
 
     def tile(s, k):
         return (s * NCH + k) * TW
 
+    def lists_of(X, o, n, v, vj, deps, depj):
+        return [V(lambda q: q.tensor_scalar(X[:, o:o + n + 2], v, HALF, None, ALU.add), n, deps),
+                S(lambda q: q.activation(X[:, o + 2 * n + 2:o + 3 * n + 4], v, ACT.Identity, bias=1 + HALF - 1 / 128), n, deps)
+                if RIGHT[o // TW] == "s" else
+                V(lambda q: q.tensor_scalar(X[:, o + 2 * n + 2:o + 3 * n + 4], v, 1 + HALF - 1 / 128, None, ALU.add), n, deps),
+                V(lambda q: q.tensor_scalar(X[:, o + n + 2:o + 2 * n + 2], vj, HALF, 4095.0, ALU.add, ALU.min), n, depj)]
+
     s0 = SET(T.ST[:, 0:4], 0, 4)
-    t0 = V(lambda q: q.tensor_tensor(T.T0[:, 0, :], T.ST[:, 4:36], T.JI[:, 0, :], ALU.add), 64, [lds, ldj])
+    t1 = V(lambda q: q.tensor_scalar(T.SX[:, :], T.ST[:, :], 127, None, ALU.bitwise_and), 36, [lds, s0])
+    t2 = V(lambda q: q.tensor_scalar(T.T0[:, 1, :], T.SX[:, :], -1 / 128, 1.0, ALU.mult, ALU.add), 36, [t1])
+    t3 = V(lambda q: q.tensor_tensor(T.T0[:, 2, :], T.T0[:, 1, :], T.ST[:, :], ALU.add), 72, [t2])
+    t0 = V(lambda q: q.tensor_tensor(T.T0[:, 0, 0:32], T.T0[:, 2, 4:36], T.JI[:, :], ALU.add), 64, [t3, ldj])
     have = {}
     for k, (c0, c1) in enumerate(CH):
-        n, o = c1 - c0, tile(0, k)
-        have[(0, k)] = [V(lambda q, n=n, o=o, c0=c0: q.tensor_copy(T.OFF[:, o:o + n + 2], T.ST[:, c0 + 2:c0 + n + 4]), n, [s0, lds]),
-                        V(lambda q, n=n, o=o, c0=c0: q.tensor_scalar(T.OFF[:, o + n + 2:o + 2 * n + 2], T.T0[:, 0, c0:c0 + n], 0.0, 4095.0,
-                                                                     ALU.max, ALU.min), n, [t0])]
+        have[(0, k)] = lists_of(T.OFF, tile(0, k), c1 - c0, T.T0[:, 2, c0 + 2:c1 + 4], T.T0[:, 0, c0:c1], [t3], [t0])
     bank = {}
-    red_last = {}
-    hist = {}
+    red_last, scans = {}, {}
 
-    def pick(out, x, n, deps):
-        return S(lambda q: q.activation(out, x, ACT.Identity), n, deps)
+    def pick(out, x, n, deps, bias=0.0):
+        return S(lambda q: q.activation(out, x, ACT.Identity, bias=bias), n, deps)
 
     def step(s, k, scan_up, pre):
         tag[0] = k
         c0, c1 = CH[k]
         n, o = c1 - c0, tile(s, k)
         last = s == N - 1
-        ns = 6 if last else 4
-        SQ, KC, RS = (T.SQ6, T.KC6, T.RS6) if last else (T.SQ4, T.KC4, T.RS4)
+        ns = 7 if last else 5
+        SQ = T.SQ
+        KC, RS = (T.KC7, T.RS7) if last else (T.KC5, T.RS5)
         fe, ui = (s - DELTA[s]) % N, UOFF.index(DELTA[s])
         Fr, Uq = F[fe], T.U[:, ui, 16 * c0:16 * c1]
         lists = have[(s, k)]
-        own, jumped = (lists[0], lists[1]) if len(lists) == 2 else (lists, lists)
-        bk, bs, bu, bd = 1 + k, 3 + k, 5 + k, 7 * k
-        BK, BS, BU, BD = T["B%d" % bk], T["B%d" % bs], T["B%d" % bu], T["B%d" % bd]
+        own, right, jumped = (lists * 3)[:3]
+        bk, bu, bs = [(1 + k, 3 + k, 5 + k), (1 + k, 4 + k, 7), (1 + k, 5 + k % 2, 7)][NCH - 2]
+        BK, BS, BU = T["B%d" % bk], T["B%d" % bs], T["B%d" % bu]
         D = [T.D[:, (s * 4 + j) * 512 + 16 * c0:(s * 4 + j) * 512 + 16 * c1] for j in range(4)]
         D[2] = T.D1[:, s * NCH + k, 0:16 * n]
-        P0, P1, P2, P3 = T.PH[:, o + 2:o + n + 2], T.PH[:, o + 1:o + n + 1], T.PH[:, o:o + n], T.PH[:, o + n + 2:o + 2 * n + 2]
-        fo = s * 96 + 3 * c0
-        Y0, Y1, Fd = T.FL[:, fo:fo + n], T.FL[:, fo + n:fo + 2 * n], T.FL[:, fo + 2 * n:fo + 3 * n]
+        o3, o1 = o + n + 2, o + 2 * n + 2
+        P0, P2, P3 = T.PH[:, o + 2:o + n + 2], T.PH[:, o:o + n], T.PH[:, o3:o3 + n]
+        Q0, Q1 = T.PH[:, o1 + 2:o1 + n + 2], T.PH[:, o1 + 1:o1 + n + 1]
+        Fd, Y2, Y1, Y0, Y3 = [T.FL[:, o + a:o + a + n] for a in (0, n, n + 1, n + 2, 2 * n + 2)]
+        nf = n if last else 3 * n + 2
 
         def gather(out, win, off, u, deps):
-            return V(lambda q: q.tensor_tensor(out, win.indirect(off), u, ALU.subtract), 16 * n, [own, frdy[fe], urdy[DELTA[s]], deps], True)
+            return V(lambda q: q.tensor_tensor(out, win.indirect(off), u, ALU.subtract), 16 * n, [frdy[fe], urdy[DELTA[s]], deps], True)
 
         def square(j, x, deps):
-            return S(lambda q: q.activation(SQ[:, c0:c1, 16 * j:16 * j + 16], x, ACT.Square), 16 * n, [deps, red_last.get((ns, k))])
+            return S(lambda q: q.activation(SQ[:, c0:c1, 16 * j:16 * j + 16], x, ACT.Square), 16 * n, [deps, red_last.get(k)])
 
-        cvt = V(lambda q: q.tensor_scalar(T.PH[:, o:o + 2 * n + 2], T.OFF[:, o:o + 2 * n + 2], -2048.0, None, ALU.add), n, [lists])
-        stk = MM([(BS[:, 0:3 * n], bI, T.SC[:, :, 0:n], True, False), (BS[:, 0:n], hS, P0, False, False), (BS[:, 0:n], hW, P1, False, False),
-                  (BS[:, n:2 * n], hS, P0, False, False), (BS[:, n:2 * n], hW, P1, False, False), (BS[:, 2 * n:3 * n], hI32, P2, False, True)],
-                 [cvt, sc, w["bI"], w["hS"], w["hW"], w["hI32"], bank.get(bs)])
-        rnd = S(lambda q: q.activation(T.FL[:, fo:fo + 3 * n], BS[:, 0:3 * n], ACT.Identity, bias=18496.015625), 3 * n, [stk])
+        wide = 3 * n + 4 + (3 * n if last else 0)
+        if HALVES[s * NCH + k] == "s":
+            cvt = pick(T.PH[:, o:o + wide], T.OFF[:, o:o + wide], wide, [lists], -2048.0)
+        else:
+            cvt = V(lambda q: q.tensor_scalar(T.PH[:, o:o + wide], T.OFF[:, o:o + wide], -2048.0, None, ALU.add), wide // 2, [lists])
+        stk = MM([(BS[:, 0:nf], bI, T.SC[:, 32 - n:32 - n + nf], True, False), (BS[:, 0:n], W["hI32"], P2, False, last)]
+                 + ([] if last else [(BS[:, n:nf], W["hI"], T.PH[:, o:o1], False, True)]),
+                 [cvt, sc, w["bI"], w["hI32"], w["hI"], bank.get(bs)])
+        rnd = S(lambda q: q.activation(T.FL[:, o:o + nf], BS[:, 0:nf], ACT.Identity, bias=18496.015625), nf, [stk])
         bank[bs] = [rnd]
-        g0 = gather(D[3], Fr[:, 0:4096], T.OFF[:, o + 2:o + n + 2], Uq, [])
-        g2 = gather(D[1], Fr[:, 128:FW], T.OFF[:, o:o + n], Uq, [])
-        g1 = gather(T.D1[:, s * NCH + k, 1:16 * n + 1], T["FS%d" % fe][:, 0:4096], T.OFF[:, o + 2:o + n + 2],
-                    T.U[:, ui, 16 * c0 + 1:16 * c1 + 1], [srdy[fe], pads])
-        g3 = S(lambda q: q.activation(D[0], Fr[:, 0:4096].indirect(T.OFF[:, o + n + 2:o + 2 * n + 2]), ACT.Copy), 16 * n, [jumped, frdy[fe]], True)
-        u1 = MM([(BU[:, 0:16 * n], bIn, Uq, True, False)], [urdy[DELTA[s]], w["bIn"], bank.get(bu)])
-        u2 = MM([(BU[:, 0:16 * n], bI, D[0], False, True)], [g3, w["bI"]], [u1])
-        q3 = square(0, BU[:, 0:16 * n], [u2])
-        bank[bu] = [q3]
+        g0 = gather(D[3], Fr[:, 0:4096], T.OFF[:, o + 2:o + n + 2], Uq, [own])
+        g2 = gather(D[1], Fr[:, 128:FW], T.OFF[:, o:o + n], Uq, [own])
+        g1 = gather(T.D1[:, s * NCH + k, 1:16 * n + 1], Fr[:, 0:4096], T.OFF[:, o1 + 2:o1 + n + 2],
+                    T.U[:, ui, 16 * c0 + 1:16 * c1 + 1], [right, pads])
+        if JUMPED[s * NCH + k] == "s":
+            g3 = S(lambda q: q.activation(D[0], Fr[:, 0:4096].indirect(T.OFF[:, o3:o3 + n]), ACT.Copy), 16 * n, [jumped, frdy[fe]], True)
+            u1 = MM([(BU[:, 0:16 * n], bIn, Uq, True, False)], [urdy[DELTA[s]], w["bIn"], bank.get(bu)])
+            u2 = MM([(BU[:, 0:16 * n], bI, D[0], False, True)], [g3, w["bI"]], [u1])
+            q3 = square(0, BU[:, 0:16 * n], [u2])
+            bank[bu] = [q3]
+        else:
+            q3 = square(0, D[0], [gather(D[0], Fr[:, 0:4096], T.OFF[:, o3:o3 + n], Uq, [jumped])])
         sq = [q3, square(3, D[3], [g0]), square(1, D[1], [g2]), square(2, D[2], [g1])]
-        K, DL, DF = BK[:, 0:ns * n], BD[:, 192:192 + ns * n], BD[:, 320:320 + ns * n]
+        K, DL, DF = BK[:, 0:ns * n], BK[:, 160:160 + ns * n], BK[:, 320:320 + ns * n]
 
         def sl(base, j):
-            return (BD if base else BK)[:, base + j:base + ns * n:ns]
+            return BK[:, base + j:base + ns * n:ns]
 
-        def part(terms, deps, after, base=192, stop=False):
-            return MM([(sl(base, j), a, x, False, stop and i == len(terms) - 1) for i, (j, a, x) in enumerate(terms)], deps, after)
+        def part(terms, deps, after, base=160):
+            return MM([(sl(base, j), a, x, False, False) for (j, a, x) in terms], deps, after)
 
-        first = T.C6[:, 0, ns * c0:ns * c1] if last else T.C4[:, ns * c0:ns * c1]
-        d = MM([(DL, bI, first, True, False)], [c6 if last else c4, w["bI"], bank.get(bd)])
+        first = T.C7[:, 0, 7 * c0:7 * c1] if last else T.C5[:, 5 * c0:5 * c1]
+        d = MM([(K, bI, KC[:, ns * c0:ns * c1], True, False), (DL, bI, first, False, False)],
+               [kc[ns], c7 if last else c5, w["bI"], bank.get(bk)])
+        parts = []
         if last:
-            bp = T.M4[:, 2, 4 * c0 + 3:4 * c1:4]
-            d = part([(4, fIn, bp), (5, fI, bp)], [pre, w["fI"], w["fIn"]], [d])
-        d = part([(0, hI, P3), (0, hIn, P2), (1, hI, P2), (4 if last else 3, hI, P0)], [cvt, w["hI"], w["hIn"]], [d])
-        d = part([(1, hSn, P0), (1, hWn, P1), (2, hSI, P0), (2, hW, P1)], [w["hSn"], w["hWn"], w["hSI"], w["hW"]], [d])
-        d = part([(0, bI, Fd), (1, bIn, Fd), (1, bq, Y1)], [rnd, w["bIn"], w["bq"], w["bqn"]], [d])
-        d = part([(1, bqn, Y0), (2, bqn, Y1), (2, bq, Y0)], [], [d], stop=True)
+            bc, bp, bf = [T.M3[:, j, 3 * c0 + 2:3 * c1:3] for j in (0, 2, 3)]
+            c4, c3, p3 = [T.PH[:, o1 + j * n + 2:o1 + (j + 1) * n + 2] for j in (1, 2, 3)]
+            hI, hIn = W["hI"], W["hIn"]
+            parts.append(part([(5, hIn, bp), (6, hI, bp)], [pre], [d]))
+            parts.append(MM([(DF, bI, T.C7[:, 1, ns * c0:ns * c1], False, False), (sl(320, 5), hIn, bf, False, False),
+                             (sl(320, 6), hI, bf, False, False)], [pre], [d]))
+            parts.append(part([(6, hI, bc)], [pre], [d], 0))
+            parts.append(part([(4, hI, c4), (5, hI, c3)], [cvt, w["hI"]], [d], 0))
+            parts.append(part([(4, hIn, p3), (5, hI, p3)], [cvt, w["hI"], w["hIn"]], [d]))
+        else:
+            je = (s + 1 - DELTA[s]) % N
+            parts.append(part([(4, bI, T.JF[:, JOFF.index(je), a + c0:a + c1]) for a in (0, 32)], [jrdy[je]], [d]))
         if last:
-            bf = T.M4[:, 3, 4 * c0 + 3:4 * c1:4]
-            d = MM([(DF, bI, T.C6[:, 1, ns * c0:ns * c1], True, False), (sl(320, 4), fIn, bf, False, False)], [], [d])
-            d = part([(5, fI, bf)], [], [d], 320, True)
-        dl = d
-        d = MM([(K, bI, KC[:, ns * c0:ns * c1], True, False)], [kc[ns], w["bI"], bank.get(bk)])
-        if last:
-            d = part([(5, fI, T.M4[:, 0, 4 * c0 + 3:4 * c1:4])], [pre, w["fI"]], [d], 0)
-            d = part([(4, fI, T.HL[:, s - 1, c0:c1])], [hist[(s - 1, k)]], [d], 0)
-        red = MM([(K, T.Z[:, 15 - r:143 - r], SQ[:, c0:c1, r::16], False, r == 15) for r in range(16)], [sq, zr, sqz[ns]], [d])
-        red_last[(ns, k)] = red
+            now = [(0, "hI", P3), (0, "hIn", P2), (1, "hI", P2), (1, "hSn", Q0), (1, "hWn", Q1), (2, "hS", Q0), (2, "hW", Q1),
+                   (2, "hIn", P0), (4, "hI", P0)]
+            later = [(0, "bI", Fd), (1, "bIn", Fd)]
+        else:
+            now = [(0, "hIa", P3), (0, "hIan", P2), (1, "hIa", P2), (1, "hSan", Q0), (1, "hWan", Q1), (2, "hSa", Q0), (2, "hWa", Q1),
+                   (2, "hIan", P0), (3, "hIa", P0)]
+            later = [(0, "bI", Fd), (1, "bIn", Fd), (0, "bIq", Y3), (0, "bIqn", Y2), (1, "bIq", Y2), (1, "bSqn", Y0), (1, "bWqn", Y1),
+                     (2, "bSI", Y0), (2, "bWq", Y1), (3, "bIq", Y0)]
+        for terms, dep in [(now, cvt), (later, rnd)]:
+            for i in range(0, len(terms), 4):
+                parts.append(part([(j, W[a], x) for j, a, x in terms[i:i + 4]], [dep, [w[a] for j, a, x in terms[i:i + 4]]], [d]))
+        red = MM([(K, T.Z[:, 15 - r:143 - r], SQ[:, c0:c1, r:16 * ns:16], False, r == 15) for r in range(16)], [sq, zr, sqz[ns]], [parts])
+        red_last[k] = red
         M, NE = T.M[:, s, ns * c0:ns * c1], T.NE[:, s, ns * c0:ns * c1]
-        R = T.R[:, s, 8 + ns * c0:8 + ns * c1]
+        R = T.R[:, s, 10 + ns * c0:10 + ns * c1]
         m1 = V(lambda q: q.tensor_tensor_scan(M, RS[:, ns * c0:ns * c1], K, 0.0, ALU.max, ALU.min), ns * n, [red, rs[ns]])
         ne = V(lambda q: q.tensor_tensor(NE, K, M, ALU.not_equal), ns * n, [m1])
-        m2 = V(lambda q: q.tensor_tensor_scan(R, NE, DL, 0.0, ALU.mult, ALU.add), ns * n, [ne, dl])
-        bank[bk] = [ne]
-        bank[bd] = [m2]
+        m2 = V(lambda q: q.tensor_tensor_scan(R, NE, DL, 0.0, ALU.mult, ALU.add), ns * n, [ne])
+        bank[bk] = [m2]
         if last:
-            m3 = V(lambda q: q.tensor_tensor_scan(T.RF[:, ns * c0:ns * c1], NE, DF, 0.0, ALU.mult, ALU.add), ns * n, [ne, dl])
-            yc = pick(T.Y[:, 0, c0:c1], T.M[:, s, ns * c0 + 5:ns * c1:ns], n, [m1])
-            yp = pick(T.Y[:, 2, c0:c1], T.R[:, s, 8 + ns * c0 + 5:8 + ns * c1:ns], n, [m2])
-            yf = V(lambda q: q.tensor_copy(T.Y[:, 1, c0:c1], T.RF[:, ns * c0 + 5:ns * c1:ns]), n, [m3])
+            m3 = V(lambda q: q.tensor_tensor_scan(T.RF[:, ns * c0:ns * c1], NE, DF, 0.0, ALU.mult, ALU.add), ns * n, [ne])
+            yc = pick(T.Y[:, 0, c0:c1], T.M[:, s, ns * c0 + 6:ns * c1:ns], n, [m1])
+            yf = pick(T.Y[:, 1, c0:c1], T.RF[:, ns * c0 + 6:ns * c1:ns], n, [m3])
+            yp = V(lambda q: q.tensor_copy(T.Y[:, 2, c0:c1], T.R[:, s, 10 + ns * c0 + 6:10 + ns * c1:ns]), n, [m2])
             DMA("y", T.yc[:, c0:c1], T.Y[:, 0, c0:c1], [yc])
-            DMA("s", T.yp[:, c0:c1], T.Y[:, 2, c0:c1], [yp])
-            DMA("y", T.yf[:, c0:c1], T.Y[:, 1, c0:c1], [yf])
+            DMA("y", T.yp[:, c0:c1], T.Y[:, 2, c0:c1], [yp])
+            DMA("s" if k == NCH - 1 else "y", T.yf[:, c0:c1], T.Y[:, 1, c0:c1], [yf])
             return m2
         hop = (DELTA[s + 1] - DELTA[s]) % N
-        je = (s + 1 - DELTA[s]) % N
-        X, o2 = (T.OFS if hop else T.OFF), tile(s + 1, k)
-        TJ = T.T0[:, s + 1, c0:c1]
-        xj = V(lambda q: q.tensor_tensor(TJ, T.R[:, s, 4 * c0 + 11:4 * c1 + 8:4], T.JI[:, JOFF.index(je), c0:c1], ALU.add), 2 * n, [m2, jrdy[je]])
-        x1 = V(lambda q: q.tensor_copy(X[:, o2:o2 + n + 2], T.R[:, s, 4 * c0 + 3:4 * c1 + 8:4]), n, [m2, scan_up, rh])
-        x2 = V(lambda q: q.tensor_scalar(X[:, o2 + n + 2:o2 + 2 * n + 2], TJ, 0.0, 4095.0, ALU.max, ALU.min), n, [xj])
-        if hop:
-            have[(s + 1, k)] = [SEND(rc(hop), T.OFF[:, o2:o2 + 2 * n + 2], T.OFS[:, o2:o2 + 2 * n + 2], "ao%d_%d" % (s + 1, k), [x1, x2])]
-        else:
-            have[(s + 1, k)] = [x1, x2]
+        o2 = tile(s + 1, k)
+        made = lists_of(T.OFS if hop else T.OFF, o2, n, T.R[:, s, 5 * c0 + 3:5 * c1 + 9:5], T.R[:, s, 5 * c0 + 14:5 * c1 + 10:5],
+                        [m2, scan_up, rh], [m2])
+        end = o2 + 3 * n + 4
+        scans[(s, k)] = m2
         if s == N - 2:
-            H = T.HS if DELTA[s] else T.HL
-            hh = pick(H[:, s, c0:c1], T.M[:, s, 4 * c0 + 3:4 * c1:4], n, [m1])
-            hist[(s, k)] = SEND(rc(-DELTA[s]), T.HL[:, s, c0:c1], T.HS[:, s, c0:c1], "ah%d_%d" % (s, k), [hh]) if DELTA[s] else hh
+            made += [pick(T.OFS[:, end:end + n], T.M[:, s, 5 * c0 + 3:5 * c1:5], n, [m1]),
+                     pick(T.OFS[:, end + n:end + 2 * n], T.M[:, s - 1, 5 * c0 + 3:5 * c1:5], n, [scans[(s - 1, k)]]),
+                     pick(T.OFS[:, end + 2 * n:end + 3 * n], T.R[:, s - 1, 5 * c0 + 13:5 * c1 + 10:5], n, [scans[(s - 1, k)]], HALF)]
+            end += 3 * n
+        if hop:
+            made = [SEND(rc(hop), T.OFF[:, o2:end], T.OFS[:, o2:end], "ao%d_%d" % (s + 1, k), made, after=[early])]
+        have[(s + 1, k)] = made
         return m2
 
     pre = None
-    old = []
+    old, oc, op = {}, {}, {}
+    home = {b - 1: (a, b) for a, b, x in runs(DELTA[:N - 3])}
     for s in range(N):
         if s == N - 1:
             B0 = T.B0
-            lst = [(B0[:, 128 + j:256:4], fI, T.HL[:, 3 - j, 32:64], j == 0, False) for j in range(4)]
-            lst += [(B0[:, 128 + j:256:4], fIn, T.HL[:, 2 - j, 32:64], False, j == 2) for j in range(3)]
-            lst += [(B0[:, j:128:4], fI, T.HL[:, 3 - j, 0:32], j == 0, j == 3) for j in range(4)]
-            pm = MM(lst[0:1], [old, w["fI"], w["fIn"], bank.get(0)])
-            for one in lst[1:]:
-                pm = MM([one], [], [pm])
-            p1 = V(lambda q: q.tensor_tensor_scan(T.M4[:, 0, :], T.RS4[:, :], B0[:, 0:128], 0.0, ALU.max, ALU.min), 128, [pm, rs[4]])
-            p2 = V(lambda q: q.tensor_tensor(T.M4[:, 1, :], B0[:, 0:128], T.M4[:, 0, :], ALU.not_equal), 128, [p1])
-            pre = [V(lambda q: q.tensor_tensor_scan(T.M4[:, 2, :], T.M4[:, 1, :], B0[:, 128:256], 0.0, ALU.mult, ALU.add), 128, [p2]),
-                   V(lambda q: q.tensor_tensor_scan(T.M4[:, 3, :], T.M4[:, 1, :], T.F4[:, :], 0.0, ALU.mult, ALU.add), 128, [p2, f4])]
-            bank[0] = pre
+            pm = None
+            for j in range(3):
+                lst = [(B0[:, 98 - j:192:3], W["hI"], op[j], j == 0, False), (B0[:, 2 - j:96:3], W["hI"], oc[j], False, j == 2)]
+                lst += [(B0[:, 97 - j:192:3], W["hIn"], op[j], False, False)] if j < 2 else []
+                pm = MM(lst, [old[j], w["hI"], w["hIn"]], [pm])
+            p1 = V(lambda q: q.tensor_tensor_scan(T.M3[:, 0, :], T.RS3[:, :], B0[:, 0:96], 0.0, ALU.max, ALU.min), 96, [pm, rs[3]])
+            p2 = V(lambda q: q.tensor_tensor(T.M3[:, 1, :], B0[:, 0:96], T.M3[:, 0, :], ALU.not_equal), 96, [p1])
+            pre = [V(lambda q: q.tensor_tensor_scan(T.M3[:, 2, :], T.M3[:, 1, :], B0[:, 96:192], 0.0, ALU.mult, ALU.add), 96, [p2]),
+                   V(lambda q: q.tensor_tensor_scan(T.M3[:, 3, :], T.M3[:, 1, :], T.F3[:, :], 0.0, ALU.mult, ALU.add), 96, [p2, f3])]
         up, ups = None, []
         for k in range(NCH):
             up = step(s, k, up, pre)
             ups.append(up)
         tag[0] = None
         if s == 0:
+            for a in range(NPC - HELD, NPC):
+                direct(frame_order()[0], a, a + 1)
+            for e in jorder[1:]:
+                jumps(e, [prev["g"]])
             for e in visits[1:]:
-                queries(e)
-        if s < N - 2:
+                queries(e, [prev["g"]])
+        if s in home:
+            a, b = home[s]
+            m = 32 * (b - a)
             H = T.HS if DELTA[s] else T.HL
-            hh = [pick(H[:, s, 0:32], T.M[:, s, 3:128:4], 32, ups), pick(H[:, s, 32:64], T.R[:, s, 11:136:4], 32, ups)]
-            old.append(SEND(rc(-DELTA[s]), T.HL[:, s, :], T.HS[:, s, :], "ah%d_0" % s, hh) if DELTA[s] else hh)
+            back = [pick(H[:, s, 0:m], T.M[:, a:b, 3:160:5], m, ups), pick(H[:, s, m:2 * m], T.R[:, a:b, 13:170:5], m, ups, HALF)]
+            if DELTA[s]:
+                back = SEND(rc(-DELTA[s]), T.HL[:, s, 0:2 * m], T.HS[:, s, 0:2 * m], "ah%d" % s, back, lat=6.0)
+            back = pick(T.HH[:, s, 0:2 * m], T.HL[:, s, 0:2 * m], 2 * m, [back], -2048.0)
+            for j in range(a, b):
+                old[j] = back
+                oc[j], op[j] = T.HH[:, s, 32 * (j - a):32 * (j - a + 1)], T.HH[:, s, m + 32 * (j - a):m + 32 * (j - a + 1)]
     return ops, sent[0]
 
 

import math
from concourse.mybir import AluOpType, AxisListType, ActivationFunctionType

N = 6
DELTA = [0, 1, 1, 3, 3, 0]
CH = [(0, 16), (16, 32)]
WAYS = "ffrr"
LATE = "ffFF"
HELD = 0
HALF = -129 / 256
HALVES = "ssssssssssss"
RIGHT = "ssssssssssss"
JUMPED = "ssssssssssss"
PASSES = 600
ROUNDS = 30000
FW = 4224
TW = 128
BIG = 8192.0
EST = {"cy": 0.9e-3, "ga": 1.56, "pe": 0.5e-3, "wake": 0.13, "hop": 2.4, "frame": 14.5, "next": 10.0}
SPREAD = [{}, {"pe": 0.7e-3, "wake": 0.1, "hop": 2.0, "frame": 13.0}, {"wake": 0.2, "pe": 0.45e-3, "hop": 3.0, "frame": 16.0}, {"cy": 1.15e-3, "ga": 1.9, "wake": 0.1}]

NCH = len(CH)
NPC = len(WAYS)
FOFF = sorted(set((s - DELTA[s]) % N for s in range(N)))
UOFF = sorted(set(DELTA))
JOFF = sorted(set([0] + [(s + 1 - DELTA[s]) % N for s in range(N - 1)]))
PW = FW // NPC

SCRATCH = {
    "U": ("sbuf", [128, len(UOFF), 528], "bfloat16"),
    "ST": ("sbuf", [128, 36], "int32"),
    "JI": ("sbuf", [128, 32], "int32"),
    "JF": ("sbuf", [128, len(JOFF), 64], "bfloat16"),
    "C5": ("sbuf", [128, 160], "bfloat16"),
    "C7": ("sbuf", [128, 2, 224], "bfloat16"),
    "T0": ("sbuf", [128, 3, 36], "float32"),
    "OFF": ("sbuf", [128, N * NCH * TW], "uint16"),
    "OFS": ("sbuf", [128, N * NCH * TW], "uint16"),
    "PH": ("sbuf", [128, N * NCH * TW], "float16"),
    "FL": ("sbuf", [128, N * NCH * TW], "bfloat16"),
    "D": ("sbuf", [128, N * 4 * 512], "bfloat16"),
    "D1": ("sbuf", [128, N * NCH, 336], "bfloat16"),
    "SQ": ("sbuf", [128, 32, 112], "bfloat16"),
    "M": ("sbuf", [128, N, 224], "float32"),
    "NE": ("sbuf", [128, N, 224], "float32"),
    "RS5": ("sbuf", [128, 160], "float32"),
    "R": ("sbuf", [128, N, 240], "float32"),
    "RF": ("sbuf", [128, 224], "float32"),
    "M3": ("sbuf", [128, 4, 96], "float16"),
    "F3": ("sbuf", [128, 96], "float32"),
    "RS3": ("sbuf", [128, 96], "float32"),
    "RS7": ("sbuf", [128, 224], "float32"),
    "KC5": ("sbuf", [128, 160], "bfloat16"),
    "KC7": ("sbuf", [128, 224], "bfloat16"),
    "SC": ("sbuf", [128, 136], "bfloat16"),
    "HS": ("sbuf", [128, N, 256], "uint16"),
    "HL": ("sbuf", [128, N, 256], "uint16"),
    "HH": ("sbuf", [128, N, 256], "float16"),
    "Y": ("sbuf", [128, 3, 32], "float32"),
    "A": ("sbuf", [128, 3, 128], "float32"),
    "E": ("sbuf", [128, 4, 8], "float32"),
    "Z": ("sbuf", [128, 144], "bfloat16"),
    "WH": ("sbuf", [128, 13, 128], "float16"),
    "SX": ("sbuf", [128, 36], "int32"),
    "WB": ("sbuf", [128, 8, 128], "bfloat16"),
}
for _e in FOFF:
    SCRATCH["FR%d" % _e] = ("sbuf", [128, FW], "bfloat16")
for _b in range(8):
    SCRATCH["B%d" % _b] = ("psum", [128, 512], "float32")

SEMAPHORES = (["cv", "cs", "ct", "cg", "ls"] + ["d%d" % i for i in range(40)]
              + ["ao%d_%d" % (s, k) for s in range(N) for k in range(NCH)]
              + ["ah%d" % s for s in range(N)]
              + ["au%d" % e for e in UOFF] + ["aj%d" % e for e in JOFF]
              + ["af%d_%d" % (e, p) for e in FOFF for p in range(NPC)] + ["al%d" % p for p in range(NPC)])

ALU = AluOpType
ACT = ActivationFunctionType
KEPT = {}


def bits(engs):
    m = 0
    for e in engs:
        m |= 1 << e
    return m


def frame_order():
    out = []
    for s in range(N):
        e = (s - DELTA[s]) % N
        if e and e not in out:
            out.append(e)
    return out


def runs(keys):
    out = []
    for p, x in enumerate(keys):
        if out and out[-1][2] == x:
            out[-1] = (out[-1][0], p + 1, x)
        else:
            out.append((p, p + 1, x))
    return out


def forwarders(T, topo, q):
    c = T.cores[q]
    dsts = [T.cores[(q - e) % N] for e in frame_order()]
    ok = [h for h in topo.cores_of(c) if T.rank_of(h) is None and all(topo.may_write(h, d) for d in dsts)]
    far = [h for h in ok if topo.die(h) != topo.die(c)]
    near = [h for h in ok if topo.die(h) == topo.die(c)]
    on = [y for y in topo.engines(c, far[0]) if "r" not in WAYS or y not in topo.engines(c, dsts[0])]
    return {"f": far[0], "F": far[-1], "n": near[0], "r": c}, on


def again():
    if len(frame_order()) < 2:
        return []
    return [x for x in runs([b if a != b else None for a, b in zip(WAYS, LATE)]) if x[2] is not None]


def sends(x):
    return runs(LATE) if x else [(p, p + 1, WAYS[p]) for p in range(NPC)]


def helper_program(g, core, T, topo):
    sent = 0
    for q in range(N):
        hs, on = forwarders(T, topo, q)
        for x, e in enumerate(frame_order()):
            dst = T.cores[(q - e) % N]
            rid, pid, _ = topo.addr(dst)
            for a, b, who in sends(x):
                if hs[who] != core:
                    continue
                if x == 0:
                    g.wait_ge(T.sem["af0_%d" % a], len(on))
                if x == 1:
                    for a2, b2, who2 in again():
                        if hs[who2] == core and a2 < b and a < b2:
                            g.wait_ge(T.sem["al%d" % a2], len(on))
                g.remote_dma(T["FR%d" % e][:, a * PW:b * PW], T.FR0[:, a * PW:b * PW], T.sem["af%d_%d" % (e, a)],
                             T.sem.ls, pid, rid, topo.mask(core, dst))
                sent += len(topo.engines(core, dst))
    if sent:
        g.wait_ge(T.sem.ls, sent)


def times(o, est):
    fix, what, n = o["cost"]
    dur = fix + n * {"c": est["cy"], "g": est["cy"] * est["ga"], "p": est["pe"]}[what]
    return dur, (est["hop"] if o["lat"] is None else o["lat"]), (est["frame"] + o["at"] if o["at"] is not None else 0.0)


def place(order, before, eng, dur, early):
    st, busy = [0.0] * len(eng), {}
    for i in order:
        t = early[i]
        for j, gap in before[i]:
            if st[j] + gap > t:
                t = st[j] + gap
        if eng[i]:
            b = busy.setdefault(eng[i], [])
            k = len(b)
            while k and b[k - 1][1] > t:
                k -= 1
            while k < len(b) and b[k][0] < t + dur[i] - 1e-9:
                t = max(t, b[k][1])
                k += 1
            b.insert(k, (t, t + dur[i]))
        st[i] = t
    return st


def schedule(ops, est, rnd):
    n = len(ops)
    tm = [times(o, est) for o in ops]
    eng, dur, tail = [o["eng"] for o in ops], [x[0] for x in tm], [x[1] for x in tm]
    early = [max(0.0, x[2] - x[0] - x[1]) for x in tm]
    fw = [[(d, dur[d] + tail[d] + est["wake"]) for d in o["deps"]] + [(d, dur[d]) for d in o["after"]] for o in ops]
    bw = [[] for _ in ops]
    for i in range(n):
        for d, gap in fw[i]:
            bw[d].append((i, gap - dur[d] + dur[i]))

    def turn(st, links, way):
        key = [-(st[i] + dur[i]) + ((rnd(201) - 100) / 500 if rnd(5) == 0 else 0.0) for i in range(n)]
        for i in range(n)[::way]:
            for j, _ in links[i]:
                key[i] = max(key[i], key[j])
        return sorted(range(n), key=lambda i: (key[i], way * i))

    back = place(range(n - 1, -1, -1), bw, [None] * n, dur, tail)
    best = cur = (1e9, None)
    for _ in range(PASSES):
        st = place(turn(back, fw, 1), fw, eng, dur, early)
        end = max(st[i] + dur[i] + tail[i] for i in range(n))
        if end < cur[0] + 0.3:
            cur = (end, st)
        if end < best[0]:
            best = (end, st)
        back = place(turn(cur[1], bw, -1), bw, eng, dur, tail)
    return sorted(range(n), key=lambda i: (round(best[1][i], 6), i))


def play(seq, ops, tm, wake):
    fin, st, free = [0.0] * len(ops), [0.0] * len(ops), {}
    for i in seq:
        o = ops[i]
        e = o["eng"]
        t = free.get(e, 0.0) if e else 0.0
        for d in o["deps"]:
            if fin[d] + wake > t:
                t = fin[d] + wake
        a, b, c = tm[i]
        st[i] = t
        fin[i] = t + a + b if t + a + b > c else c
        if e:
            free[e] = t + a
    return max(fin), st


def improve(ops):
    n = len(ops)
    cases = []
    for kw in SPREAD:
        est = dict(EST)
        est.update(kw)
        cases.append(([times(o, est) for o in ops], est["wake"]))

    def cost(s):
        return sum(play(s, ops, tm, wk)[0] for tm, wk in cases) / len(cases)

    pre = [set(o["deps"] + o["after"]) for o in ops]
    x = [12345]

    def rnd(m):
        x[0] = (x[0] * 1103515245 + 12345) % 2147483648
        return (x[0] >> 8) % m

    cur, seq = min((cost(s), s) for s in [schedule(ops, EST, rnd) for _ in range(4)])
    best, kept = cur, seq

    for it in range(ROUNDS):
        if it % 300 == 0:
            st = play(seq, ops, cases[0][0], cases[0][1])[1]
            pos = {j: k for k, j in enumerate(seq)}
            seq = sorted(seq, key=lambda j: (round(st[j], 6), pos[j]))
        a = rnd(n)
        e = ops[seq[a]]["eng"]
        if e is None:
            continue
        k, way, b, seen, grp = [1, 1, 1, 2, 3, 5][rnd(6)], 2 * rnd(2) - 1, a, 0, [seq[a]]
        while seen < k:
            b += way
            if b < 0 or b >= n:
                break
            j = seq[b]
            if any(j in pre[y] for y in grp) if way < 0 else any(y in pre[j] for y in grp):
                if ops[j]["eng"] == e:
                    break
                grp.append(j)
            elif ops[j]["eng"] == e:
                seen += 1
        if seen < k:
            continue
        lo, hi = min(a, b), max(a, b)
        mine, rest = [m for m in seq[lo:hi + 1] if m in grp], [m for m in seq[lo:hi + 1] if m not in grp]
        c = seq[:lo] + (mine + rest if way < 0 else rest + mine) + seq[hi + 1:]
        v = cost(c)
        if v <= cur or rnd(1000000) < 1000000 * math.exp((cur - v) / (0.03 * (1 - it / ROUNDS) + 1e-4)):
            seq, cur = c, v
            if v < best:
                best, kept = v, c
    return kept


def build(g, core, T, topo, rank):
    ops = []
    nd = [0]
    sent = [0]
    tag = [None]
    prev = {}

    def flat(x):
        out = []
        for d in x:
            if isinstance(d, (list, tuple)):
                out += flat(d)
            elif d is not None:
                out.append(d)
        return out

    def add(eng, fn, cost, deps=(), after=(), kind="c", lat=0.0, sem=None, val=0, at=None):
        ops.append({"eng": eng, "fn": fn, "cost": cost, "deps": sorted(set(flat(deps))), "after": sorted(set(flat(after))),
                    "kind": kind, "lat": lat, "sem": sem, "val": val, "at": at, "tag": tag[0]})
        return len(ops) - 1

    def V(fn, n, deps=(), gather=False):
        return add("v", fn, (0.05, "g", n) if gather else (0.01, "c", max(n, 64)), deps)

    def S(fn, n, deps=(), gather=False):
        return add("s", fn, (0.065, "g", n) if gather else (0.03, "c", max(n, 64)), deps)

    def MM(lst, deps=(), after=()):
        def fn(q):
            for (o, w, x, a, b) in lst:
                ins = q.matmul(o, w, x, a, b)
            return ins
        cyc = 0
        for (o, w, x, a, b) in lst:
            cyc += max(64, list(o.shape)[1]) * (4 if "32" in str(w.dtype) else 1)
        return add("t", fn, (0.0, "p", cyc), deps, after)

    def DMA(eng, out, in_, deps=(), lat=2.0):
        name = "d%d" % nd[0]
        nd[0] += 1
        prev[eng] = add(eng, lambda q: q.dma_start(out, in_), (0.1, "c", 0), deps, [prev.get(eng)], kind="d", lat=lat, sem=name, val=16)
        return prev[eng]

    def WRITE(dst, out, in_, sem, deps, engs, after=()):
        rid, pid, _ = topo.addr(dst)
        sent[0] += len(engs)
        prev["g"] = add("g", lambda q: q.remote_dma(out, in_, T.sem[sem], T.sem.ls, pid, rid, bits(engs)), (0.3, "c", 0), deps, after, kind="r")
        return prev["g"]

    def LAND(i, sem, got, lat=None, at=None):
        return add(None, None, (0.0, "c", 0), [i], kind="a", lat=lat, sem=sem, val=got, at=at)

    def SEND(dst, out, in_, sem, deps, lat=None, after=()):
        engs = topo.engines(core, dst)
        return LAND(WRITE(dst, out, in_, sem, deps, engs, after), sem, len(engs), lat)

    def rc(k):
        return T.cores[(rank + k) % N]

    F = {e: T["FR%d" % e] for e in FOFF}
    ldj = DMA("y", T.JI[:, :], T.ju[:, :])
    lds = DMA("y", T.ST[:, 4:36], T.st[:, :])
    ldu = DMA("s", T.U[:, 0, 0:512], T.qu[:, :], lat=2.3)
    ldf = []
    for p in range(NPC):
        a, b = p * PW, min((p + 1) * PW, 4096)
        one = [DMA("y" if p % 2 == 0 else "s", F[0][:, a:b], T.fr[:, a:b], lat=2.8 + 2.4 * p / (NPC - 1))]
        if p == NPC - 1:
            one.append(DMA("y", F[0][:, 4096:FW], T.fr[:, 3968:4096], lat=3.0))
        ldf.append(one)
    jh = V(lambda q: q.tensor_copy(T.JF[:, 0, 0:32], T.JI[:, :]), 32, [ldj])
    jrdy = {0: V(lambda q: q.tensor_tensor(T.JF[:, 0, 32:64], T.JI[:, :], T.JF[:, 0, 0:32], ALU.subtract), 64, [jh])}
    urdy = {0: ldu}
    visits = sorted(UOFF[1:], key=DELTA.index)
    jorder = sorted(JOFF[1:], key=[(s + 1 - DELTA[s]) % N for s in range(N - 1)].index)

    def jumps(e, after):
        jrdy[e] = SEND(rc(-e), T.JF[:, JOFF.index(e), :], T.JF[:, 0, :], "aj%d" % e, [jrdy[0]], lat=4.0, after=after)

    def queries(e, after):
        urdy[e] = SEND(rc(e), T.U[:, UOFF.index(e), 0:512], T.U[:, 0, 0:512], "au%d" % e, [ldu], lat=4.0, after=after)

    jumps(jorder[0], [])
    queries(visits[0], [prev["g"]])
    frdy = {e: [] for e in FOFF}
    frdy[0] = ldf
    hs, on = forwarders(T, topo, rank)

    def direct(e, a, b):
        frdy[e].append(SEND(rc(-e), F[e][:, a * PW:b * PW], F[0][:, a * PW:b * PW], "af%d_%d" % (e, a), ldf[a:b], lat=4.0, after=[prev["g"]]))

    for x, e in enumerate(frame_order()):
        for a, b, who in (again() if x == 1 else []):
            piece = F[0][:, a * PW:b * PW]
            WRITE(hs[who], piece, piece, "al%d" % a, ldf[a:b], on, [prev["g"]])
        for a, b, who in sends(x):
            piece = F[0][:, a * PW:b * PW]
            if hs[who] == core:
                if a < NPC - HELD:
                    direct(e, a, b)
                continue
            if x == 0:
                WRITE(hs[who], piece, piece, "af0_%d" % a, ldf[a:b], on, [prev["g"]])
            frdy[e].append(LAND(prev["g"], "af%d_%d" % (e, a), len(topo.engines(forwarders(T, topo, (rank + e) % N)[0][who], core)),
                                at=x * EST["next"]))
    early = prev["g"]

    def IOTA(out, pat, n):
        return add("g", lambda q: q.iota(out, pat, 0, -1, allow_small_or_imprecise_dtypes=True), (0.13, "c", 2 * n))

    def SET(ap, val, n, deps=()):
        return V(lambda q: q.memset(ap, val), n, deps)

    def EQ(out, a, val, mul, deps):
        return V(lambda q: q.tensor_scalar(out, a, float(val), float(mul), ALU.is_equal, ALU.mult), 128, deps)

    ia = IOTA(T.A[:, 0, :], [[1, 128]], 128)
    ib = IOTA(T.A[:, 1, :], [[1, 128]], 128)
    ic = IOTA(T.A[:, 2, :], [[16, 8], [200, 16]], 128)
    ie = IOTA(T.E[:, 0, :], [[16, 8]], 8)
    ib2 = SET(T.A[:, 1, 0::16], 999.0, 8, [ib])
    A0, A1, A2 = T.A[:, 0, :], T.A[:, 1, :], T.A[:, 2, :]
    W, w, used = {}, {}, {"h": 0, "b": 0, "f": 0}
    al, qu = 127 / 128, 1 / 128
    for name, mul in [("hI", 1), ("hI32", 1 / 32), ("bI", 1), ("bIn", -1), ("hIa", al), ("hIan", -al), ("hSa", al), ("hSan", -al),
                      ("hWa", al), ("hWan", -al), ("bIq", qu), ("bIqn", -qu), ("bSqn", -qu), ("bWq", qu), ("bWqn", -qu), ("bSI", None),
                      ("hIn", -1), ("hS", 1), ("hW", 1), ("hSn", -1), ("hWn", -1)]:
        W[name] = {"h": T.WH, "b": T.WB}[name[0]][:, used[name[0]], :]
        used[name[0]] += 1
        if mul is not None:
            src, val, dep = {"I": (A0, 0, ia), "S": (A1, 1, ib2), "W": (A2, -15, ic)}[name[1]]
            w[name] = EQ(W[name], src, val, mul, [dep])
    w["bSI"] = V(lambda q: q.tensor_tensor(W["bSI"], W["bIqn"], W["bSqn"], ALU.subtract), 128, [w["bIqn"], w["bSqn"]])
    bI, bIn = W["bI"], W["bIn"]
    pads = [SET(T.U[:, :, 512:528], 0.0, 24), SET(T.D1[:, :, 0:1], 0.0, 12)]
    z0 = SET(T.Z[:, :], 0.0, 72)
    e1 = S(lambda q: q.activation(T.E[:, 1, :], T.E[:, 0, :], ACT.Abs, bias=7.5), 8, [ie])
    zr = V(lambda q: q.tensor_scalar(T.Z[:, 15:143:16], T.E[:, 1, :], 8.0, None, ALU.is_lt), 8, [z0, e1])
    e2 = V(lambda q: q.tensor_scalar(T.E[:, 2, :], T.E[:, 0, :], 0.0, BIG, ALU.is_equal, ALU.mult), 8, [ie])
    e3 = V(lambda q: q.tensor_reduce(T.E[:, 3, 0:1], T.E[:, 2, :], AxisListType.X, ALU.add), 8, [e2])
    kc, rs = {}, {}
    for ns, KC in [(5, T.KC5), (7, T.KC7)]:
        k0 = SET(KC[:, :], 0.0, 16 * ns)
        kc[ns] = [SET(KC[:, 1:2 * ns:ns], BIG, 2, [k0]),
                  V(lambda q, KC=KC, ns=ns: q.tensor_scalar(KC[:, 2::2 * ns], KC[:, 3::2 * ns], T.E[:, 3, 0:1], None, ALU.add), 16, [k0, e3])]
    kc[5].append(SET(T.KC5[:, 4::5], 2 * BIG, 32, [kc[5]]))
    kc[7] += [SET(T.KC7[:, j::7], 2048.0, 32, [kc[7]]) for j in (4, 5, 6)]
    for ns, RS in [(3, T.RS3), (5, T.RS5), (7, T.RS7)]:
        rs[ns] = SET(RS[:, 0::ns], 4 * BIG, 32, [SET(RS[:, :], -BIG, 32 * ns)])
    sqz = {5: [SET(T.SQ[:, a:a + 16, 64:80], 0.0, 128) for a in (0, 16)]}
    sqz[7] = sqz[5] + [SET(T.SQ[:, a:a + 8, 80:112], 0.0, 128) for a in range(0, 32, 8)]
    sc = [SET(T.SC[:, 0:32], -60.0, 16), SET(T.SC[:, 32:104], 0.5, 36)]
    rh = SET(T.R[:, :, 0:10], 0.0, 60)
    c50 = SET(T.C5[:, :], 0.0, 80)
    c5 = [SET(T.C5[:, k::5], v, 32, [c50]) for k, v in [(0, -18560.0), (1, 18560.0), (3, 1904.0)]]
    fn_ = [float((rank + s) % N) for s in range(N)]
    c70 = SET(T.C7[:, :, :], 0.0, 224)
    c7 = [SET(T.C7[:, a, k::7], v, 32, [c70]) for a, k, v in
          [(0, 0, -18560.0), (0, 1, 18560.0), (0, 6, 2048.0), (1, 3, fn_[5] - fn_[4]), (1, 4, fn_[4] - fn_[3]), (1, 5, fn_[3])]]
    f3 = [SET(T.F3[:, k::3], v, 32) for k, v in enumerate([fn_[2] - fn_[1], fn_[1] - fn_[0], fn_[0]])]

    def tile(s, k):
        return (s * NCH + k) * TW

    def lists_of(X, o, n, v, vj, deps, depj):
        return [V(lambda q: q.tensor_scalar(X[:, o:o + n + 2], v, HALF, None, ALU.add), n, deps),
                S(lambda q: q.activation(X[:, o + 2 * n + 2:o + 3 * n + 4], v, ACT.Identity, bias=1 + HALF - 1 / 128), n, deps)
                if RIGHT[o // TW] == "s" else
                V(lambda q: q.tensor_scalar(X[:, o + 2 * n + 2:o + 3 * n + 4], v, 1 + HALF - 1 / 128, None, ALU.add), n, deps),
                V(lambda q: q.tensor_scalar(X[:, o + n + 2:o + 2 * n + 2], vj, HALF, 4095.0, ALU.add, ALU.min), n, depj)]

    s0 = SET(T.ST[:, 0:4], 0, 4)
    t1 = V(lambda q: q.tensor_scalar(T.SX[:, :], T.ST[:, :], 127, None, ALU.bitwise_and), 36, [lds, s0])
    t2 = V(lambda q: q.tensor_scalar(T.T0[:, 1, :], T.SX[:, :], -1 / 128, 1.0, ALU.mult, ALU.add), 36, [t1])
    t3 = V(lambda q: q.tensor_tensor(T.T0[:, 2, :], T.T0[:, 1, :], T.ST[:, :], ALU.add), 72, [t2])
    t0 = V(lambda q: q.tensor_tensor(T.T0[:, 0, 0:32], T.T0[:, 2, 4:36], T.JI[:, :], ALU.add), 64, [t3, ldj])
    have = {}
    for k, (c0, c1) in enumerate(CH):
        have[(0, k)] = lists_of(T.OFF, tile(0, k), c1 - c0, T.T0[:, 2, c0 + 2:c1 + 4], T.T0[:, 0, c0:c1], [t3], [t0])
    bank = {}
    red_last, scans = {}, {}

    def pick(out, x, n, deps, bias=0.0):
        return S(lambda q: q.activation(out, x, ACT.Identity, bias=bias), n, deps)

    def step(s, k, scan_up, pre):
        tag[0] = k
        c0, c1 = CH[k]
        n, o = c1 - c0, tile(s, k)
        last = s == N - 1
        ns = 7 if last else 5
        SQ = T.SQ
        KC, RS = (T.KC7, T.RS7) if last else (T.KC5, T.RS5)
        fe, ui = (s - DELTA[s]) % N, UOFF.index(DELTA[s])
        Fr, Uq = F[fe], T.U[:, ui, 16 * c0:16 * c1]
        lists = have[(s, k)]
        own, right, jumped = (lists * 3)[:3]
        bk, bu, bs = [(1 + k, 3 + k, 5 + k), (1 + k, 4 + k, 7), (1 + k, 5 + k % 2, 7)][NCH - 2]
        BK, BS, BU = T["B%d" % bk], T["B%d" % bs], T["B%d" % bu]
        D = [T.D[:, (s * 4 + j) * 512 + 16 * c0:(s * 4 + j) * 512 + 16 * c1] for j in range(4)]
        D[2] = T.D1[:, s * NCH + k, 0:16 * n]
        o3, o1 = o + n + 2, o + 2 * n + 2
        P0, P2, P3 = T.PH[:, o + 2:o + n + 2], T.PH[:, o:o + n], T.PH[:, o3:o3 + n]
        Q0, Q1 = T.PH[:, o1 + 2:o1 + n + 2], T.PH[:, o1 + 1:o1 + n + 1]
        Fd, Y2, Y1, Y0, Y3 = [T.FL[:, o + a:o + a + n] for a in (0, n, n + 1, n + 2, 2 * n + 2)]
        nf = n if last else 3 * n + 2

        def gather(out, win, off, u, deps):
            return V(lambda q: q.tensor_tensor(out, win.indirect(off), u, ALU.subtract), 16 * n, [frdy[fe], urdy[DELTA[s]], deps], True)

        def square(j, x, deps):
            return S(lambda q: q.activation(SQ[:, c0:c1, 16 * j:16 * j + 16], x, ACT.Square), 16 * n, [deps, red_last.get(k)])

        wide = 3 * n + 4 + (3 * n if last else 0)
        if HALVES[s * NCH + k] == "s":
            cvt = pick(T.PH[:, o:o + wide], T.OFF[:, o:o + wide], wide, [lists], -2048.0)
        else:
            cvt = V(lambda q: q.tensor_scalar(T.PH[:, o:o + wide], T.OFF[:, o:o + wide], -2048.0, None, ALU.add), wide // 2, [lists])
        stk = MM([(BS[:, 0:nf], bI, T.SC[:, 32 - n:32 - n + nf], True, False), (BS[:, 0:n], W["hI32"], P2, False, last)]
                 + ([] if last else [(BS[:, n:nf], W["hI"], T.PH[:, o:o1], False, True)]),
                 [cvt, sc, w["bI"], w["hI32"], w["hI"], bank.get(bs)])
        rnd = S(lambda q: q.activation(T.FL[:, o:o + nf], BS[:, 0:nf], ACT.Identity, bias=18496.015625), nf, [stk])
        bank[bs] = [rnd]
        g0 = gather(D[3], Fr[:, 0:4096], T.OFF[:, o + 2:o + n + 2], Uq, [own])
        g2 = gather(D[1], Fr[:, 128:FW], T.OFF[:, o:o + n], Uq, [own])
        g1 = gather(T.D1[:, s * NCH + k, 1:16 * n + 1], Fr[:, 0:4096], T.OFF[:, o1 + 2:o1 + n + 2],
                    T.U[:, ui, 16 * c0 + 1:16 * c1 + 1], [right, pads])
        if JUMPED[s * NCH + k] == "s":
            g3 = S(lambda q: q.activation(D[0], Fr[:, 0:4096].indirect(T.OFF[:, o3:o3 + n]), ACT.Copy), 16 * n, [jumped, frdy[fe]], True)
            u1 = MM([(BU[:, 0:16 * n], bIn, Uq, True, False)], [urdy[DELTA[s]], w["bIn"], bank.get(bu)])
            u2 = MM([(BU[:, 0:16 * n], bI, D[0], False, True)], [g3, w["bI"]], [u1])
            q3 = square(0, BU[:, 0:16 * n], [u2])
            bank[bu] = [q3]
        else:
            q3 = square(0, D[0], [gather(D[0], Fr[:, 0:4096], T.OFF[:, o3:o3 + n], Uq, [jumped])])
        sq = [q3, square(3, D[3], [g0]), square(1, D[1], [g2]), square(2, D[2], [g1])]
        K, DL, DF = BK[:, 0:ns * n], BK[:, 160:160 + ns * n], BK[:, 320:320 + ns * n]

        def sl(base, j):
            return BK[:, base + j:base + ns * n:ns]

        def part(terms, deps, after, base=160):
            return MM([(sl(base, j), a, x, False, False) for (j, a, x) in terms], deps, after)

        first = T.C7[:, 0, 7 * c0:7 * c1] if last else T.C5[:, 5 * c0:5 * c1]
        d = MM([(K, bI, KC[:, ns * c0:ns * c1], True, False), (DL, bI, first, False, False)],
               [kc[ns], c7 if last else c5, w["bI"], bank.get(bk)])
        parts = []
        if last:
            bc, bp, bf = [T.M3[:, j, 3 * c0 + 2:3 * c1:3] for j in (0, 2, 3)]
            c4, c3, p3 = [T.PH[:, o1 + j * n + 2:o1 + (j + 1) * n + 2] for j in (1, 2, 3)]
            hI, hIn = W["hI"], W["hIn"]
            parts.append(part([(5, hIn, bp), (6, hI, bp)], [pre], [d]))
            parts.append(MM([(DF, bI, T.C7[:, 1, ns * c0:ns * c1], False, False), (sl(320, 5), hIn, bf, False, False),
                             (sl(320, 6), hI, bf, False, False)], [pre], [d]))
            parts.append(part([(6, hI, bc)], [pre], [d], 0))
            parts.append(part([(4, hI, c4), (5, hI, c3)], [cvt, w["hI"]], [d], 0))
            parts.append(part([(4, hIn, p3), (5, hI, p3)], [cvt, w["hI"], w["hIn"]], [d]))
        else:
            je = (s + 1 - DELTA[s]) % N
            parts.append(part([(4, bI, T.JF[:, JOFF.index(je), a + c0:a + c1]) for a in (0, 32)], [jrdy[je]], [d]))
        if last:
            now = [(0, "hI", P3), (0, "hIn", P2), (1, "hI", P2), (1, "hSn", Q0), (1, "hWn", Q1), (2, "hS", Q0), (2, "hW", Q1),
                   (2, "hIn", P0), (4, "hI", P0)]
            later = [(0, "bI", Fd), (1, "bIn", Fd)]
        else:
            now = [(0, "hIa", P3), (0, "hIan", P2), (1, "hIa", P2), (1, "hSan", Q0), (1, "hWan", Q1), (2, "hSa", Q0), (2, "hWa", Q1),
                   (2, "hIan", P0), (3, "hIa", P0)]
            later = [(0, "bI", Fd), (1, "bIn", Fd), (0, "bIq", Y3), (0, "bIqn", Y2), (1, "bIq", Y2), (1, "bSqn", Y0), (1, "bWqn", Y1),
                     (2, "bSI", Y0), (2, "bWq", Y1), (3, "bIq", Y0)]
        for terms, dep in [(now, cvt), (later, rnd)]:
            for i in range(0, len(terms), 4):
                parts.append(part([(j, W[a], x) for j, a, x in terms[i:i + 4]], [dep, [w[a] for j, a, x in terms[i:i + 4]]], [d]))
        red = MM([(K, T.Z[:, 15 - r:143 - r], SQ[:, c0:c1, r:16 * ns:16], False, r == 15) for r in range(16)], [sq, zr, sqz[ns]], [parts])
        red_last[k] = red
        M, NE = T.M[:, s, ns * c0:ns * c1], T.NE[:, s, ns * c0:ns * c1]
        R = T.R[:, s, 10 + ns * c0:10 + ns * c1]
        m1 = V(lambda q: q.tensor_tensor_scan(M, RS[:, ns * c0:ns * c1], K, 0.0, ALU.max, ALU.min), ns * n, [red, rs[ns]])
        ne = V(lambda q: q.tensor_tensor(NE, K, M, ALU.not_equal), ns * n, [m1])
        m2 = V(lambda q: q.tensor_tensor_scan(R, NE, DL, 0.0, ALU.mult, ALU.add), ns * n, [ne])
        bank[bk] = [m2]
        if last:
            m3 = V(lambda q: q.tensor_tensor_scan(T.RF[:, ns * c0:ns * c1], NE, DF, 0.0, ALU.mult, ALU.add), ns * n, [ne])
            yc = pick(T.Y[:, 0, c0:c1], T.M[:, s, ns * c0 + 6:ns * c1:ns], n, [m1])
            yf = pick(T.Y[:, 1, c0:c1], T.RF[:, ns * c0 + 6:ns * c1:ns], n, [m3])
            yp = V(lambda q: q.tensor_copy(T.Y[:, 2, c0:c1], T.R[:, s, 10 + ns * c0 + 6:10 + ns * c1:ns]), n, [m2])
            DMA("y", T.yc[:, c0:c1], T.Y[:, 0, c0:c1], [yc])
            DMA("y", T.yp[:, c0:c1], T.Y[:, 2, c0:c1], [yp])
            DMA("s" if k == NCH - 1 else "y", T.yf[:, c0:c1], T.Y[:, 1, c0:c1], [yf])
            return m2
        hop = (DELTA[s + 1] - DELTA[s]) % N
        o2 = tile(s + 1, k)
        made = lists_of(T.OFS if hop else T.OFF, o2, n, T.R[:, s, 5 * c0 + 3:5 * c1 + 9:5], T.R[:, s, 5 * c0 + 14:5 * c1 + 10:5],
                        [m2, scan_up, rh], [m2])
        end = o2 + 3 * n + 4
        scans[(s, k)] = m2
        if s == N - 2:
            made += [pick(T.OFS[:, end:end + n], T.M[:, s, 5 * c0 + 3:5 * c1:5], n, [m1]),
                     pick(T.OFS[:, end + n:end + 2 * n], T.M[:, s - 1, 5 * c0 + 3:5 * c1:5], n, [scans[(s - 1, k)]]),
                     pick(T.OFS[:, end + 2 * n:end + 3 * n], T.R[:, s - 1, 5 * c0 + 13:5 * c1 + 10:5], n, [scans[(s - 1, k)]], HALF)]
            end += 3 * n
        if hop:
            made = [SEND(rc(hop), T.OFF[:, o2:end], T.OFS[:, o2:end], "ao%d_%d" % (s + 1, k), made, after=[early])]
        have[(s + 1, k)] = made
        return m2

    pre = None
    old, oc, op = {}, {}, {}
    home = {b - 1: (a, b) for a, b, x in runs(DELTA[:N - 3])}
    for s in range(N):
        if s == N - 1:
            B0 = T.B0
            pm = None
            for j in range(3):
                lst = [(B0[:, 98 - j:192:3], W["hI"], op[j], j == 0, False), (B0[:, 2 - j:96:3], W["hI"], oc[j], False, j == 2)]
                lst += [(B0[:, 97 - j:192:3], W["hIn"], op[j], False, False)] if j < 2 else []
                pm = MM(lst, [old[j], w["hI"], w["hIn"]], [pm])
            p1 = V(lambda q: q.tensor_tensor_scan(T.M3[:, 0, :], T.RS3[:, :], B0[:, 0:96], 0.0, ALU.max, ALU.min), 96, [pm, rs[3]])
            p2 = V(lambda q: q.tensor_tensor(T.M3[:, 1, :], B0[:, 0:96], T.M3[:, 0, :], ALU.not_equal), 96, [p1])
            pre = [V(lambda q: q.tensor_tensor_scan(T.M3[:, 2, :], T.M3[:, 1, :], B0[:, 96:192], 0.0, ALU.mult, ALU.add), 96, [p2]),
                   V(lambda q: q.tensor_tensor_scan(T.M3[:, 3, :], T.M3[:, 1, :], T.F3[:, :], 0.0, ALU.mult, ALU.add), 96, [p2, f3])]
        up, ups = None, []
        for k in range(NCH):
            up = step(s, k, up, pre)
            ups.append(up)
        tag[0] = None
        if s == 0:
            for a in range(NPC - HELD, NPC):
                direct(frame_order()[0], a, a + 1)
            for e in jorder[1:]:
                jumps(e, [prev["g"]])
            for e in visits[1:]:
                queries(e, [prev["g"]])
        if s in home:
            a, b = home[s]
            m = 32 * (b - a)
            H = T.HS if DELTA[s] else T.HL
            back = [pick(H[:, s, 0:m], T.M[:, a:b, 3:160:5], m, ups), pick(H[:, s, m:2 * m], T.R[:, a:b, 13:170:5], m, ups, HALF)]
            if DELTA[s]:
                back = SEND(rc(-DELTA[s]), T.HL[:, s, 0:2 * m], T.HS[:, s, 0:2 * m], "ah%d" % s, back, lat=6.0)
            back = pick(T.HH[:, s, 0:2 * m], T.HL[:, s, 0:2 * m], 2 * m, [back], -2048.0)
            for j in range(a, b):
                old[j] = back
                oc[j], op[j] = T.HH[:, s, 32 * (j - a):32 * (j - a + 1)], T.HH[:, s, m + 32 * (j - a):m + 32 * (j - a + 1)]
    return ops, sent[0]


def rank_program(g, core, T, topo):
    rank = T.rank_of(core)
    if rank is None:
        helper_program(g, core, T, topo)
        return
    ops, sent = build(g, core, T, topo, rank)
    if "seq" not in KEPT:
        KEPT["seq"] = improve(ops)
    order = {}
    for i in KEPT["seq"]:
        order.setdefault(ops[i]["eng"], []).append(i)
    queue = {"v": g.vector, "s": g.scalar, "t": g.tensor, "y": g.sync, "g": g}
    needed = set(d for o in ops for d in o["deps"])
    total = {}
    for eng in queue:
        cnt = 0
        for i in order.get(eng, []):
            if ops[i]["kind"] == "c" and i in needed:
                cnt += 1
                ops[i]["sem"], ops[i]["val"] = "c" + eng, cnt
                total["c" + eng] = cnt
    for o in ops:
        if o["kind"] in "da":
            total[o["sem"]] = o["val"]
    for eng, q in queue.items():
        seen = {}
        for i in order.get(eng, []):
            o = ops[i]
            want = {}
            for d in o["deps"]:
                want[ops[d]["sem"]] = max(want.get(ops[d]["sem"], 0), ops[d]["val"])
            for sem, val in want.items():
                if seen.get(sem, 0) < val:
                    q.wait_ge(T.sem[sem], val)
                    seen[sem] = val
            ins = o["fn"](q)
            if o["kind"] == "d":
                ins.then_inc(T.sem[o["sem"]], 16)
            elif o["kind"] == "c" and o["sem"]:
                ins.then_inc(T.sem[o["sem"]], 1)
        if eng == "g":
            total["ls"] = sent
            for sem, val in total.items():
                if seen.get(sem, 0) < val:
                    q.wait_ge(T.sem[sem], val)
